import numpy as np
import ml_dtypes


def mxq(x, axis, fmt="e4m3"):
    dtype, down = {"e4m3": (ml_dtypes.float8_e4m3fn, 7), "e5m2": (ml_dtypes.float8_e5m2, 14)}[fmt]
    v = np.moveaxis(np.asarray(x, np.float32).astype(ml_dtypes.bfloat16).astype(np.float64), axis, -1)
    blocks = v.reshape(v.shape[:-1] + (-1, 32))
    amax = np.abs(blocks).max(-1, keepdims=True)
    byte = np.maximum(np.where(amax > 0, np.frexp(amax)[1] - 1 + 127, 0) - down, 1)
    scale = np.exp2(byte - 127.0)
    codes = (blocks / scale).astype(np.float32).astype(dtype).astype(np.float64)
    return np.moveaxis((codes * scale).reshape(v.shape), -1, axis)


WIDE = False


def mx_kscale(k):
    if not WIDE:
        return np.ones(k)
    levels = np.array([10, -10, 5, -5, 0])
    if k % 512:
        return np.exp2(np.random.permutation(np.resize(levels, k // 32))).repeat(32)
    a = np.empty((k // 512, 16))
    for p in range(k // 512):
        a[p, :8] = np.random.permutation(np.resize(levels, 8))
        for g in range(8):
            far = levels[np.abs(levels - a[p, g]) >= 10]
            a[p, g + 8] = far[np.random.randint(len(far))]
    return np.exp2(a.ravel()).repeat(32)


def f64(x):
    return np.asarray(x).astype(np.float64)


def striped(idx):
    return np.tile(idx.reshape(-1, 16).T, (8, 1)).astype(np.uint16)


def unstriped(offs):
    return offs[:16].T.reshape(-1).astype(np.int64)


E2M1 = np.array([0.0, 0.5, 1.0, 1.5, 2.0, 3.0, 4.0, 6.0, -0.0, -0.5, -1.0, -1.5, -2.0, -3.0, -4.0, -6.0])


def pack_weight(w, fmt):
    k, n = w.shape
    w = f64(np.asarray(w, np.float32).astype(ml_dtypes.bfloat16)).reshape(k // 32, 32, n)
    amax = np.abs(w).max(1)
    if fmt == "e4m3":
        byte = np.frexp(amax)[1] - 1 + 127 - 7
    else:
        mant, ex = np.frexp(amax / 6.0)
        byte = np.where(mant > 0.5, ex, ex - 1) + 127
    byte = np.clip(np.where(amax > 0, byte, 1), 1, 254)
    scaled = (w * np.exp2(127.0 - byte)[:, None, :]).reshape(k, n).astype(np.float32)
    by_word = np.ascontiguousarray(scaled.reshape(k // 512, 128, 4, n).transpose(0, 1, 3, 2))
    if fmt == "e4m3":
        words = by_word.astype(ml_dtypes.float8_e4m3fn).view(np.uint8)
    else:
        c = by_word.astype(ml_dtypes.float4_e2m1fn).view(np.uint8) & 0xF
        words = (c[..., 0::2] | (c[..., 1::2] << 4)).reshape(k // 512, 128, 2 * n)
    return np.ascontiguousarray(words), np.ascontiguousarray(byte.astype(np.uint8).reshape(k // 512, 16, n))


def unpack_weight(words, scales, fmt):
    g, _, n = scales.shape
    words = np.ascontiguousarray(words).reshape(g, 128, n, -1)
    if fmt == "e4m3":
        vals = words.view(ml_dtypes.float8_e4m3fn).astype(np.float64)
    else:
        nib = np.empty((g, 128, n, 4), np.uint8)
        nib[..., 0::2] = words & 0xF
        nib[..., 1::2] = words >> 4
        vals = E2M1[nib]
    vals = vals * np.repeat(np.exp2(scales.astype(np.float64) - 127.0), 8, axis=1)[..., None]
    return vals.transpose(0, 1, 3, 2).reshape(g * 512, n)


def gelu(v):
    return 0.5 * v * (1.0 + np.tanh(np.sqrt(2.0 / np.pi) * (v + 0.044715 * v**3)))


def bf(x):
    return np.asarray(x, np.float32).astype(ml_dtypes.bfloat16)

def planes(Y):
    n, m = Y.shape
    b = f64(bf(Y)).reshape(n // 32, 32, m)
    amax = np.abs(b).max(1)
    byte = np.clip(np.where(amax > 0, np.frexp(amax)[1] - 1 + 127 - 7, 1), 1, 254)
    codes = (b * np.exp2(127.0 - byte)[:, None, :]).reshape(n, m).astype(np.float32).astype(ml_dtypes.float8_e4m3fn).view(np.uint8)
    words = codes.reshape(n // 512, 128, 4, m).transpose(0, 1, 3, 2)
    return np.ascontiguousarray(words), np.ascontiguousarray(byte.astype(np.uint8).reshape(n // 512, 16, m))


K, N, H, T, S = 1024, 1024, 1536, 2048, 512

def setup_inputs():
    n = np.random.standard_normal
    s = mx_kscale(K)[:, None]
    u = mx_kscale(H)[:, None]
    head = n((K, H)) / np.sqrt(K)
    gain = np.exp(0.8 * n(N))
    tab_words, tab_scales = pack_weight(n((K, T)) * s, "e4m3")
    wb_words, wb_scales = pack_weight(head.T * gain[None, :] / u, "e2m1")
    offs = striped(np.random.permutation(T)[:S])
    return {
        "tab_words": tab_words,
        "tab_scales": tab_scales,
        "offs": offs,
        "a": (head / s).astype(np.float32),
        "b": (0.5 * n(H) - 0.8).astype(np.float32),
        "gT": (np.random.random((H, T)) < 0.3).astype(np.float32),
        "c": (np.exp(0.3 * n(H)) * u[:, 0]).astype(np.float32),
        "wb_words": wb_words,
        "wb_scales": wb_scales,
    }

def reference(tab_words, tab_scales, offs, a, b, gT, c, wb_words, wb_scales):
    v = unpack_weight(tab_words, tab_scales, "e4m3")[:, unstriped(offs)]
    g = f64(gT)[:, unstriped(offs)]
    wb = unpack_weight(wb_words, wb_scales, "e2m1")
    z = (mxq(f64(a), 0, "e4m3").T @ v) + f64(b)[:, None]
    p = 1.0 / (1.0 + np.exp(-z))
    d = (p - g) * f64(c)[:, None]
    y = wb.T @ mxq(d, 0, "e4m3")
    words, scales = planes(y)
    return y, words, scales

@@ -1,0 +1,209 @@
+from contextlib import ExitStack
+
+import concourse.mybir as mybir
+
+K, N, H, T, S = 1024, 1024, 1536, 2048, 512
+FLOPS = 2 * K * H * S + 2 * H * N * S
+
+F32 = mybir.dt.float32
+BF16 = mybir.dt.bfloat16
+I32 = mybir.dt.int32
+U32 = mybir.dt.uint32
+U16 = mybir.dt.uint16
+U8 = mybir.dt.uint8
+FP8X4 = mybir.dt.float8_e4m3fn_x4
+FP4X4 = mybir.dt.float4_e2m1fn_x4
+ALU = mybir.AluOpType
+ACT = mybir.ActivationFunctionType
+
+P = 128
+PACK = 4
+PASS = P * PACK
+K_PASSES = K // PASS
+R_PASSES = H // PASS
+N_GROUPS = N // PASS
+HALF = S // 2
+AHEAD = 8
+
+
+def tile_list_click_feature_grad_kernel(
+    tc, tab_words, tab_scales, offs, a, b, gT, c, wb_words, wb_scales, out_0, out_1, out_2
+):
+    nc = tc.nc
+    with ExitStack() as ctx:
+        keep = ctx.enter_context(tc.tile_pool(name="keep", bufs=1))
+        ring = ctx.enter_context(tc.tile_pool(name="ring", bufs=2))
+        psum = ctx.enter_context(tc.psum_pool(name="psum", bufs=8))
+
+        offsets = keep.tile([P, S // 16], U16, name="offsets")
+        nc.sync.dma_start(offsets[:], offs)
+
+        tab_scale_rows = keep.tile([P, T], U8, name="tab_scale_rows", align_bytes=64)
+        wb_scale_rows = keep.tile([P, R_PASSES, N], U8, name="wb_scale_rows", align_bytes=64)
+        nc.gpsimd.memset(tab_scale_rows[:].bitcast(I32), 0)
+        nc.vector.memset(wb_scale_rows[:].bitcast(I32), 0)
+
+        for q in range(4):
+            nc.scalar.dma_start(
+                tab_scale_rows[32 * q + 4 : 32 * q + 4 + 4 * K_PASSES, :].bitcast(I32),
+                tab_scales[:, 4 * q : 4 * q + 4, :].bitcast(I32),
+            )
+        bias = keep.tile([P, R_PASSES, PACK], F32, name="bias")
+        weight = keep.tile([P, R_PASSES, PACK], F32, name="weight")
+        nc.scalar.dma_start(bias[:], b.rearrange("(a p t) -> p a t", p=P, t=PACK))
+        nc.scalar.dma_start(weight[:], c.rearrange("(a p t) -> p a t", p=P, t=PACK))
+        minus_weight = keep.tile([P, R_PASSES, PACK], F32, name="minus_weight")
+
+        wb_raw = keep.tile([P, R_PASSES, 2 * N], U8, name="wb_raw", align_bytes=64)
+        wb_codes = keep.tile([P, R_PASSES, 2 * N], U8, name="wb_codes", align_bytes=64)
+        wb_planes = keep.tile([P, R_PASSES, N], U8, name="wb_planes", align_bytes=64)
+        tab = [keep.tile([P, T], I32, name="tab%d" % kp, align_bytes=64) for kp in range(K_PASSES)]
+        v_codes = [keep.tile([P, S], U32, name="v_codes%d" % kp, align_bytes=64) for kp in range(K_PASSES)]
+        v_planes = keep.tile([P, S], U8, name="v_planes", align_bytes=64)
+        d_round = [keep.tile([P, S, PACK], BF16, name="d_round%d" % rp, align_bytes=64) for rp in range(R_PASSES)]
+        a_raw, a_codes, a_planes, prob, label_rows, y_banks = {}, {}, {}, {}, {}, []
+
+        def load_tab(kp):
+            nc.sync.dma_start(tab[kp][:], tab_words[kp].rearrange("p t i -> p (t i)").bitcast(I32))
+
+        def use_tab(kp):
+            nc.vector.tensor_copy(v_codes[kp][:], tab[kp][:].bitcast(U32).indirect(offsets[:]))
+            if kp == K_PASSES - 1:
+                nc.vector.tensor_copy(v_planes[:], tab_scale_rows[:].indirect(offsets[:]))
+                nc.vector.tensor_scalar(minus_weight[:], weight[:], -1.0, None, ALU.mult)
+
+        def load_a(kp, rp):
+            a_raw[kp, rp] = ring.tile([P, PACK, PASS], F32, name="a_raw", tag="wide", bufs=5)
+            block = a[kp * PASS : (kp + 1) * PASS, rp * PASS : (rp + 1) * PASS]
+            nc.sync.dma_start(a_raw[kp, rp][:], block.rearrange("(p j) r -> p j r", j=PACK))
+
+        def use_a(kp, rp):
+            a_round = ring.tile([P, PACK * PASS], BF16, name="a_round", tag="round", align_bytes=64)
+            nc.vector.tensor_copy(
+                a_round[:].rearrange("p (t m j) -> p m j t", t=PACK, j=PACK),
+                a_raw[kp, rp][:].rearrange("p j (m t) -> p m j t", t=PACK),
+            )
+            a_codes[kp, rp] = ring.tile([P, PASS], U32, name="a_codes", bufs=4, align_bytes=64)
+            a_planes[kp, rp] = ring.tile([P, PASS], U8, name="a_planes", bufs=4, align_bytes=64)
+            nc.vector.quantize_mx(a_codes[kp, rp][:].bitcast(FP8X4), a_planes[kp, rp][:], a_round[:])
+            if kp == K_PASSES - 1:
+                for t in range(PACK):
+                    predict(rp, t)
+
+        def predict(rp, t):
+            cols = slice(t * P, (t + 1) * P)
+            logits = psum.tile([P, S], F32, name="bank")
+            for kp in range(K_PASSES):
+                nc.tensor.matmul_mx(
+                    logits[:],
+                    lhsT=a_codes[kp, rp][:, cols].bitcast(FP8X4),
+                    lhsT_scale=a_planes[kp, rp][:, cols],
+                    rhs=v_codes[kp][:].bitcast(FP8X4),
+                    rhs_scale=v_planes[4 * kp + 4 : P, :],
+                    start=(kp == 0),
+                    stop=(kp == K_PASSES - 1),
+                )
+            prob[rp, t] = keep.tile([P, S], F32, name="prob%d%d" % (rp, t), align_bytes=64)
+            nc.scalar.activation(prob[rp, t][:], logits[:], ACT.Sigmoid, bias=bias[:, rp, t : t + 1])
+
+        def load_wb():
+            nc.sync.dma_start(wb_raw[:].bitcast(I32), wb_words.rearrange("a p e -> p a e").bitcast(I32))
+
+        def use_wb():
+            for rp in range(R_PASSES):
+                nc.vector.tensor_copy(
+                    wb_codes[:, rp, :].bitcast(U16).rearrange("p (g t m) -> p g m t", g=N_GROUPS, t=PACK),
+                    wb_raw[:, rp, :].bitcast(U16).rearrange("p (g m t) -> p g m t", g=N_GROUPS, t=PACK),
+                )
+
+        def load_wb_scales(q):
+            nc.sync.dma_start(
+                wb_scale_rows[32 * q : 32 * q + 4, :, :].bitcast(I32),
+                wb_scales[:, 4 * q : 4 * q + 4, :].rearrange("a r n -> r a n").bitcast(I32),
+            )
+
+        def use_wb_scales(q):
+            if q == 3:
+                nc.vector.tensor_copy(
+                    wb_planes[:].rearrange("p a (g t m) -> p (a g) m t", g=N_GROUPS, t=PACK),
+                    wb_scale_rows[:].rearrange("p a (g m t) -> p (a g) m t", g=N_GROUPS, t=PACK),
+                )
+
+        def load_labels(rp, t):
+            label_rows[rp, t] = ring.tile([P, T], F32, name="label_rows", bufs=8)
+            rows = gT[rp * PASS : (rp + 1) * PASS, :].rearrange("(p t) x -> p t x", t=PACK)
+            nc.sync.dma_start(label_rows[rp, t][:], rows[:, t, :])
+
+        def use_labels(rp, t):
+            scale = minus_weight[:, rp, t : t + 1]
+            window = label_rows[rp, t][:]
+            if rp == R_PASSES - 1 and t >= 2:
+                first = ring.tile([P, HALF], F32, name="miss_first")
+                second = ring.tile([P, HALF], F32, name="miss_second")
+                nc.vector.tensor_tensor(first[:], window.indirect(offsets[:, : HALF // 16]), prob[rp, t][:, :HALF], ALU.subtract)
+                nc.vector.tensor_tensor(second[:], window.indirect(offsets[:, HALF // 16 :]), prob[rp, t][:, HALF:], ALU.subtract)
+                nc.scalar.activation(d_round[rp][:, :HALF, t], first[:], ACT.Copy, scale=scale)
+                nc.vector.tensor_scalar(d_round[rp][:, HALF:, t], second[:], scale, None, ALU.mult)
+            else:
+                miss = ring.tile([P, S], F32, name="miss", bufs=3)
+                nc.vector.tensor_tensor(miss[:], window.indirect(offsets[:]), prob[rp, t][:], ALU.subtract)
+                nc.scalar.activation(d_round[rp][:, :, t], miss[:], ACT.Copy, scale=scale)
+            if rp == R_PASSES - 1 and t >= 1:
+                back_project(t - 1)
+
+        def back_project(rp):
+            if rp == 0:
+                y_banks.extend(psum.tile([P, S], F32, name="bank") for i in range(N_GROUPS * PACK))
+            d_codes = keep.tile([P, S], U32, name="d_codes", tag="prob%d%d" % (R_PASSES - 1, rp + 1), align_bytes=64)
+            d_plane = keep.tile([P, S], U8, name="d_plane%d" % rp, align_bytes=64)
+            nc.vector.quantize_mx(d_codes[:].bitcast(FP8X4), d_plane[:], d_round[rp][:].rearrange("p s t -> p (s t)"))
+            for i in range(N_GROUPS * PACK):
+                nc.tensor.matmul_mx(
+                    y_banks[i][:],
+                    lhsT=wb_codes[:, rp, 2 * P * i : 2 * P * (i + 1)].bitcast(FP4X4),
+                    lhsT_scale=wb_planes[:, rp, P * i : P * (i + 1)],
+                    rhs=d_codes[:].bitcast(FP8X4),
+                    rhs_scale=d_plane[:],
+                    start=(rp == 0),
+                    stop=(rp == R_PASSES - 1),
+                )
+
+        TAB, A, WB, WS, G = (load_tab, use_tab), (load_a, use_a), (load_wb, use_wb), (load_wb_scales, use_wb_scales), (load_labels, use_labels)
+        stream = [
+            (TAB, 0), (A, 0, 0), (TAB, 1), (A, 1, 0), (G, 0, 0), (WS, 0), (A, 0, 1), (WS, 1), (G, 0, 1), (WS, 2), (A, 1, 1), (WS, 3),
+            (G, 0, 2), (A, 0, 2), (G, 1, 0), (A, 1, 2), (G, 1, 1), (WB,), (G, 1, 2), (G, 2, 0),
+            (G, 0, 3), (G, 2, 1), (G, 1, 3), (G, 2, 2), (G, 2, 3),
+        ]
+        for item in stream[:AHEAD]:
+            item[0][0](*item[1:])
+        for step, item in enumerate(stream):
+            item[0][1](*item[1:])
+            if step + AHEAD < len(stream):
+                later = stream[step + AHEAD]
+                later[0][0](*later[1:])
+
+        y_planes = keep.tile([P, N_GROUPS, S], U8, name="y_planes", align_bytes=64)
+        for g in range(N_GROUPS):
+            y = ring.tile([P, PACK, S], F32, name="y", tag="wide", bufs=5)
+            rows = out_0[g * PASS : (g + 1) * PASS, :].rearrange("(p t) j -> p t j", t=PACK)
+            for t in range(PACK):
+                bank = y_banks[g * PACK + t]
+                if g == 0 and t % 2 == 1:
+                    nc.vector.tensor_copy(y[:, t, :], bank[:])
+                else:
+                    nc.scalar.copy(y[:, t, :], bank[:])
+                nc.sync.dma_start(rows[:, t, :], y[:, t, :])
+            y_round = ring.tile([P, PACK * S], BF16, name="y_round", tag="round", align_bytes=64)
+            nc.vector.tensor_copy(
+                y_round[:].rearrange("p (u i t) -> p u t i", i=4, t=PACK),
+                y[:].rearrange("p t (u i) -> p u t i", i=4),
+            )
+            y_codes = keep.tile([P, S], U32, name="y_codes%d" % g, align_bytes=64)
+            nc.vector.quantize_mx(y_codes[:].bitcast(FP8X4), y_planes[:, g, :], y_round[:])
+            nc.sync.dma_start(out_1[g].rearrange("p m t -> p (m t)").bitcast(I32), y_codes[:].bitcast(I32))
+        for q in range(4):
+            queue = nc.sync if q % 2 == 0 else nc.scalar
+            queue.dma_start(
+                out_2[:, 4 * q : 4 * q + 4, :].rearrange("g r m -> r g m").bitcast(I32),
+                y_planes[32 * q : 32 * q + 4, :, :].bitcast(I32),
+            )

@@ -1,6 +1,7 @@
 from contextlib import ExitStack
 
 import concourse.mybir as mybir
+from concourse.masks import make_identity
 
 K, N, H, T, S = 1024, 1024, 1536, 2048, 512
 FLOPS = 2 * K * H * S + 2 * H * N * S
@@ -23,7 +24,7 @@ K_PASSES = K // PASS
 R_PASSES = H // PASS
 N_GROUPS = N // PASS
 HALF = S // 2
-AHEAD = 8
+LABEL_BUFS = 8
 
 
 def tile_list_click_feature_grad_kernel(
@@ -40,104 +41,120 @@ def tile_list_click_feature_grad_kernel(
 
         tab_scale_rows = keep.tile([P, T], U8, name="tab_scale_rows", align_bytes=64)
         wb_scale_rows = keep.tile([P, R_PASSES, N], U8, name="wb_scale_rows", align_bytes=64)
-        nc.gpsimd.memset(tab_scale_rows[:].bitcast(I32), 0)
-        nc.vector.memset(wb_scale_rows[:].bitcast(I32), 0)
+        slot_rows = keep.tile([P, PASS], F32, name="slot_rows")
+        identity = keep.tile([P, P], F32, name="identity")
+        nc.gpsimd.memset(slot_rows[:], 0.0)
+        nc.vector.memset(tab_scale_rows[:].bitcast(I32), 0)
+        nc.gpsimd.memset(wb_scale_rows[:].bitcast(I32), 0)
+        make_identity(nc, identity[:])
 
+        nc.scalar.dma_start(slot_rows[0:R_PASSES, :], b.rearrange("(a r) -> a r", r=PASS))
+        nc.scalar.dma_start(slot_rows[R_PASSES : 2 * R_PASSES, :], c.rearrange("(a r) -> a r", r=PASS))
         for q in range(4):
             nc.scalar.dma_start(
                 tab_scale_rows[32 * q + 4 : 32 * q + 4 + 4 * K_PASSES, :].bitcast(I32),
                 tab_scales[:, 4 * q : 4 * q + 4, :].bitcast(I32),
             )
-        bias = keep.tile([P, R_PASSES, PACK], F32, name="bias")
-        weight = keep.tile([P, R_PASSES, PACK], F32, name="weight")
-        nc.scalar.dma_start(bias[:], b.rearrange("(a p t) -> p a t", p=P, t=PACK))
-        nc.scalar.dma_start(weight[:], c.rearrange("(a p t) -> p a t", p=P, t=PACK))
-        minus_weight = keep.tile([P, R_PASSES, PACK], F32, name="minus_weight")
-
-        wb_raw = keep.tile([P, R_PASSES, 2 * N], U8, name="wb_raw", align_bytes=64)
-        wb_codes = keep.tile([P, R_PASSES, 2 * N], U8, name="wb_codes", align_bytes=64)
-        wb_planes = keep.tile([P, R_PASSES, N], U8, name="wb_planes", align_bytes=64)
-        tab = [keep.tile([P, T], I32, name="tab%d" % kp, align_bytes=64) for kp in range(K_PASSES)]
-        v_codes = [keep.tile([P, S], U32, name="v_codes%d" % kp, align_bytes=64) for kp in range(K_PASSES)]
-        v_planes = keep.tile([P, S], U8, name="v_planes", align_bytes=64)
-        d_round = [keep.tile([P, S, PACK], BF16, name="d_round%d" % rp, align_bytes=64) for rp in range(R_PASSES)]
-        a_raw, a_codes, a_planes, prob, label_rows, y_banks = {}, {}, {}, {}, {}, []
-
-        def load_tab(kp):
-            nc.sync.dma_start(tab[kp][:], tab_words[kp].rearrange("p t i -> p (t i)").bitcast(I32))
-
-        def use_tab(kp):
-            nc.vector.tensor_copy(v_codes[kp][:], tab[kp][:].bitcast(U32).indirect(offsets[:]))
-            if kp == K_PASSES - 1:
-                nc.vector.tensor_copy(v_planes[:], tab_scale_rows[:].indirect(offsets[:]))
-                nc.vector.tensor_scalar(minus_weight[:], weight[:], -1.0, None, ALU.mult)
-
-        def load_a(kp, rp):
-            a_raw[kp, rp] = ring.tile([P, PACK, PASS], F32, name="a_raw", tag="wide", bufs=5)
-            block = a[kp * PASS : (kp + 1) * PASS, rp * PASS : (rp + 1) * PASS]
-            nc.sync.dma_start(a_raw[kp, rp][:], block.rearrange("(p j) r -> p j r", j=PACK))
-
-        def use_a(kp, rp):
-            a_round = ring.tile([P, PACK * PASS], BF16, name="a_round", tag="round", align_bytes=64)
-            nc.vector.tensor_copy(
-                a_round[:].rearrange("p (t m j) -> p m j t", t=PACK, j=PACK),
-                a_raw[kp, rp][:].rearrange("p j (m t) -> p m j t", t=PACK),
-            )
-            a_codes[kp, rp] = ring.tile([P, PASS], U32, name="a_codes", bufs=4, align_bytes=64)
-            a_planes[kp, rp] = ring.tile([P, PASS], U8, name="a_planes", bufs=4, align_bytes=64)
-            nc.vector.quantize_mx(a_codes[kp, rp][:].bitcast(FP8X4), a_planes[kp, rp][:], a_round[:])
-            if kp == K_PASSES - 1:
-                for t in range(PACK):
-                    predict(rp, t)
-
-        def predict(rp, t):
-            cols = slice(t * P, (t + 1) * P)
-            logits = psum.tile([P, S], F32, name="bank")
-            for kp in range(K_PASSES):
-                nc.tensor.matmul_mx(
-                    logits[:],
-                    lhsT=a_codes[kp, rp][:, cols].bitcast(FP8X4),
-                    lhsT_scale=a_planes[kp, rp][:, cols],
-                    rhs=v_codes[kp][:].bitcast(FP8X4),
-                    rhs_scale=v_planes[4 * kp + 4 : P, :],
-                    start=(kp == 0),
-                    stop=(kp == K_PASSES - 1),
-                )
-            prob[rp, t] = keep.tile([P, S], F32, name="prob%d%d" % (rp, t), align_bytes=64)
-            nc.scalar.activation(prob[rp, t][:], logits[:], ACT.Sigmoid, bias=bias[:, rp, t : t + 1])
-
-        def load_wb():
-            nc.sync.dma_start(wb_raw[:].bitcast(I32), wb_words.rearrange("a p e -> p a e").bitcast(I32))
-
-        def use_wb():
-            for rp in range(R_PASSES):
-                nc.vector.tensor_copy(
-                    wb_codes[:, rp, :].bitcast(U16).rearrange("p (g t m) -> p g m t", g=N_GROUPS, t=PACK),
-                    wb_raw[:, rp, :].bitcast(U16).rearrange("p (g m t) -> p g m t", g=N_GROUPS, t=PACK),
-                )
-
-        def load_wb_scales(q):
-            nc.sync.dma_start(
+        for q in range(4):
+            nc.scalar.dma_start(
                 wb_scale_rows[32 * q : 32 * q + 4, :, :].bitcast(I32),
                 wb_scales[:, 4 * q : 4 * q + 4, :].rearrange("a r n -> r a n").bitcast(I32),
             )
 
-        def use_wb_scales(q):
-            if q == 3:
-                nc.vector.tensor_copy(
-                    wb_planes[:].rearrange("p a (g t m) -> p (a g) m t", g=N_GROUPS, t=PACK),
-                    wb_scale_rows[:].rearrange("p a (g m t) -> p (a g) m t", g=N_GROUPS, t=PACK),
-                )
+        wb_raw = keep.tile([P, R_PASSES, 2 * N], U8, name="wb_raw", align_bytes=64)
+        nc.sync.dma_start(wb_raw[:].bitcast(I32), wb_words.rearrange("a p e -> p a e").bitcast(I32))
+        a_raw = [ring.tile([P, PACK, H], F32, name="a_raw", tag="wide") for kp in range(K_PASSES)]
+        tab = [keep.tile([P, T], I32, name="tab%d" % kp, align_bytes=64) for kp in range(K_PASSES)]
+        a_rows = a.rearrange("(k p j) r -> k p j r", p=P, j=PACK)
+        nc.sync.dma_start(a_raw[0][:], a_rows[0])
+        for kp in range(K_PASSES):
+            nc.sync.dma_start(tab[kp][:], tab_words[kp].rearrange("p t i -> p (t i)").bitcast(I32))
+        nc.sync.dma_start(a_raw[1][:], a_rows[1])
+
+        order = [(0, 0), (0, 1), (0, 2), (1, 0), (1, 1), (1, 2), (2, 0), (0, 3), (2, 1), (1, 3), (2, 2), (2, 3)]
+        label_rows = {}
 
         def load_labels(rp, t):
-            label_rows[rp, t] = ring.tile([P, T], F32, name="label_rows", bufs=8)
+            label_rows[rp, t] = ring.tile([P, T], F32, name="label_rows", bufs=LABEL_BUFS)
             rows = gT[rp * PASS : (rp + 1) * PASS, :].rearrange("(p t) x -> p t x", t=PACK)
             nc.sync.dma_start(label_rows[rp, t][:], rows[:, t, :])
 
-        def use_labels(rp, t):
-            scale = minus_weight[:, rp, t : t + 1]
+        for rp, t in order[:LABEL_BUFS]:
+            load_labels(rp, t)
+
+        wb_codes = keep.tile([P, R_PASSES, 2 * N], U8, name="wb_codes", align_bytes=64)
+        nc.vector.tensor_copy(
+            wb_codes[:].bitcast(U16).rearrange("p a (g t m) -> p (a g) t m", g=N_GROUPS, t=PACK),
+            wb_raw[:].bitcast(U16).rearrange("p a (g m t) -> p (a g) t m", g=N_GROUPS, t=PACK),
+        )
+
+        turned = psum.tile([P, PACK, P], F32, name="bank")
+        for t in range(PACK):
+            nc.tensor.transpose(turned[:, t, :], slot_rows[:, t::PACK], identity[:])
+        bias = keep.tile([P, PACK, R_PASSES], F32, name="bias")
+        minus_weight = keep.tile([P, PACK, R_PASSES], F32, name="minus_weight")
+        nc.scalar.copy(bias[:], turned[:, :, 0:R_PASSES])
+        nc.scalar.activation(minus_weight[:], turned[:, :, R_PASSES : 2 * R_PASSES], ACT.Copy, scale=-1.0)
+
+        a_round, a_codes, a_planes, prob = {}, {}, {}, {}
+
+        def round_a(kp, rp):
+            a_round[kp, rp] = ring.tile([P, PACK * PASS], BF16, name="a_round", tag="round", align_bytes=64)
+            dealt = a_round[kp, rp][:].rearrange("p (u e m j) -> p u m j e", u=2, e=2, j=PACK)
+            block = a_raw[kp][:, :, rp * PASS : (rp + 1) * PASS].rearrange("p j (m u e) -> p u m j e", u=2, e=2)
+            for u in range(2):
+                nc.vector.tensor_copy(dealt[:, u], block[:, u])
+
+        def quantise_a(kp, rp):
+            a_codes[kp, rp] = keep.tile([P, PASS], U32, name="a_codes%d%d" % (kp, rp), align_bytes=64)
+            a_planes[kp, rp] = keep.tile([P, PASS], U8, name="a_planes%d%d" % (kp, rp), align_bytes=64)
+            nc.vector.quantize_mx(a_codes[kp, rp][:].bitcast(FP8X4), a_planes[kp, rp][:], a_round[kp, rp][:])
+
+        def prepare_a(kp):
+            round_a(kp, 0)
+            for rp in range(R_PASSES):
+                if rp + 1 < R_PASSES:
+                    round_a(kp, rp + 1)
+                quantise_a(kp, rp)
+
+        prepare_a(0)
+        v_codes = [keep.tile([P, S], U32, name="v_codes%d" % kp, align_bytes=64) for kp in range(K_PASSES)]
+        for kp in range(K_PASSES):
+            nc.vector.tensor_copy(v_codes[kp][:], tab[kp][:].bitcast(U32).indirect(offsets[:]))
+        v_planes = keep.tile([P, S], U8, name="v_planes", tag="tab0", align_bytes=64)
+        nc.vector.tensor_copy(v_planes[:], tab_scale_rows[:].indirect(offsets[:]))
+        wb_planes = keep.tile([P, R_PASSES, N], U8, name="wb_planes", tag="tab1", align_bytes=64)
+        nc.vector.tensor_copy(
+            wb_planes[:].rearrange("p a (g t m) -> p (a g) t m", g=N_GROUPS, t=PACK),
+            wb_scale_rows[:].rearrange("p a (g m t) -> p (a g) t m", g=N_GROUPS, t=PACK),
+        )
+        prepare_a(1)
+
+        for rp in range(R_PASSES):
+            for t in range(PACK):
+                cols = slice(t * P, (t + 1) * P)
+                logits = psum.tile([P, S], F32, name="bank")
+                for kp in range(K_PASSES):
+                    nc.tensor.matmul_mx(
+                        logits[:],
+                        lhsT=a_codes[kp, rp][:, cols].bitcast(FP8X4),
+                        lhsT_scale=a_planes[kp, rp][:, cols],
+                        rhs=v_codes[kp][:].bitcast(FP8X4),
+                        rhs_scale=v_planes[4 * kp + 4 : P, :],
+                        start=(kp == 0),
+                        stop=(kp == K_PASSES - 1),
+                    )
+                prob[rp, t] = keep.tile([P, S], F32, name="prob%d%d" % (rp, t), align_bytes=64)
+                nc.scalar.activation(prob[rp, t][:], logits[:], ACT.Sigmoid, bias=bias[:, t, rp : rp + 1])
+
+        d_round = [keep.tile([P, S, PACK], BF16, name="d_round%d" % rp, align_bytes=64) for rp in range(R_PASSES)]
+        y_banks = [psum.tile([P, S], F32, name="bank") for i in range(N_GROUPS * PACK)]
+        last = R_PASSES - 1
+
+        def logit_gradient(rp, t):
+            scale = minus_weight[:, t, rp : rp + 1]
             window = label_rows[rp, t][:]
-            if rp == R_PASSES - 1 and t >= 2:
+            if rp == last and t >= 2:
                 first = ring.tile([P, HALF], F32, name="miss_first")
                 second = ring.tile([P, HALF], F32, name="miss_second")
                 nc.vector.tensor_tensor(first[:], window.indirect(offsets[:, : HALF // 16]), prob[rp, t][:, :HALF], ALU.subtract)
@@ -147,16 +164,18 @@ def tile_list_click_feature_grad_kernel(
             else:
                 miss = ring.tile([P, S], F32, name="miss", bufs=3)
                 nc.vector.tensor_tensor(miss[:], window.indirect(offsets[:]), prob[rp, t][:], ALU.subtract)
-                nc.scalar.activation(d_round[rp][:, :, t], miss[:], ACT.Copy, scale=scale)
-            if rp == R_PASSES - 1 and t >= 1:
-                back_project(t - 1)
+                if rp == 0 and t < 2:
+                    nc.vector.tensor_scalar(d_round[rp][:, :, t], miss[:], scale, None, ALU.mult)
+                else:
+                    nc.scalar.activation(d_round[rp][:, :, t], miss[:], ACT.Copy, scale=scale)
 
         def back_project(rp):
-            if rp == 0:
-                y_banks.extend(psum.tile([P, S], F32, name="bank") for i in range(N_GROUPS * PACK))
-            d_codes = keep.tile([P, S], U32, name="d_codes", tag="prob%d%d" % (R_PASSES - 1, rp + 1), align_bytes=64)
+            d_codes = keep.tile([P, S], U32, name="d_codes", tag="prob%d%d" % (last, rp + 1), align_bytes=64)
             d_plane = keep.tile([P, S], U8, name="d_plane%d" % rp, align_bytes=64)
-            nc.vector.quantize_mx(d_codes[:].bitcast(FP8X4), d_plane[:], d_round[rp][:].rearrange("p s t -> p (s t)"))
+            for cols in [slice(0, HALF), slice(HALF, S)] if rp == last else [slice(0, S)]:
+                nc.vector.quantize_mx(
+                    d_codes[:, cols].bitcast(FP8X4), d_plane[:, cols], d_round[rp][:, cols, :].rearrange("p s t -> p (s t)")
+                )
             for i in range(N_GROUPS * PACK):
                 nc.tensor.matmul_mx(
                     y_banks[i][:],
@@ -165,45 +184,53 @@ def tile_list_click_feature_grad_kernel(
                     rhs=d_codes[:].bitcast(FP8X4),
                     rhs_scale=d_plane[:],
                     start=(rp == 0),
-                    stop=(rp == R_PASSES - 1),
+                    stop=(rp == last),
                 )
 
-        TAB, A, WB, WS, G = (load_tab, use_tab), (load_a, use_a), (load_wb, use_wb), (load_wb_scales, use_wb_scales), (load_labels, use_labels)
-        stream = [
-            (TAB, 0), (A, 0, 0), (TAB, 1), (A, 1, 0), (G, 0, 0), (WS, 0), (A, 0, 1), (WS, 1), (G, 0, 1), (WS, 2), (A, 1, 1), (WS, 3),
-            (G, 0, 2), (A, 0, 2), (G, 1, 0), (A, 1, 2), (G, 1, 1), (WB,), (G, 1, 2), (G, 2, 0),
-            (G, 0, 3), (G, 2, 1), (G, 1, 3), (G, 2, 2), (G, 2, 3),
-        ]
-        for item in stream[:AHEAD]:
-            item[0][0](*item[1:])
-        for step, item in enumerate(stream):
-            item[0][1](*item[1:])
-            if step + AHEAD < len(stream):
-                later = stream[step + AHEAD]
-                later[0][0](*later[1:])
+        for step, (rp, t) in enumerate(order):
+            logit_gradient(rp, t)
+            if step + LABEL_BUFS < len(order):
+                load_labels(*order[step + LABEL_BUFS])
+            if rp == last and t >= 1:
+                back_project(t - 1)
 
         y_planes = keep.tile([P, N_GROUPS, S], U8, name="y_planes", align_bytes=64)
-        for g in range(N_GROUPS):
-            y = ring.tile([P, PACK, S], F32, name="y", tag="wide", bufs=5)
+        y, y_round = [], []
+
+        def empty_banks(g):
+            y.append(ring.tile([P, PACK, S], F32, name="y", tag="wide"))
             rows = out_0[g * PASS : (g + 1) * PASS, :].rearrange("(p t) j -> p t j", t=PACK)
             for t in range(PACK):
                 bank = y_banks[g * PACK + t]
-                if g == 0 and t % 2 == 1:
-                    nc.vector.tensor_copy(y[:, t, :], bank[:])
+                if (g == 0 and t % 2 == 1) or (g == 1 and t == 3):
+                    nc.vector.tensor_copy(y[g][:, t, :], bank[:])
                 else:
-                    nc.scalar.copy(y[:, t, :], bank[:])
-                nc.sync.dma_start(rows[:, t, :], y[:, t, :])
-            y_round = ring.tile([P, PACK * S], BF16, name="y_round", tag="round", align_bytes=64)
+                    nc.scalar.copy(y[g][:, t, :], bank[:])
+                if g == 0 and t < 2:
+                    nc.sync.dma_start(rows[:, t, :], y[g][:, t, :])
+                elif t % 2 == 1:
+                    nc.sync.dma_start(rows[:, t - 1 : t + 1, :], y[g][:, t - 1 : t + 1, :])
+
+        def round_y(g):
+            y_round.append(ring.tile([P, PACK * S], BF16, name="y_round", tag="round", align_bytes=64))
             nc.vector.tensor_copy(
-                y_round[:].rearrange("p (u i t) -> p u t i", i=4, t=PACK),
-                y[:].rearrange("p t (u i) -> p u t i", i=4),
+                y_round[g][:].rearrange("p (u i t) -> p u t i", i=4, t=PACK),
+                y[g][:].rearrange("p t (u i) -> p u t i", i=4),
             )
+
+        def quantise_y(g):
             y_codes = keep.tile([P, S], U32, name="y_codes%d" % g, align_bytes=64)
-            nc.vector.quantize_mx(y_codes[:].bitcast(FP8X4), y_planes[:, g, :], y_round[:])
+            nc.vector.quantize_mx(y_codes[:].bitcast(FP8X4), y_planes[:, g, :], y_round[g][:])
             nc.sync.dma_start(out_1[g].rearrange("p m t -> p (m t)").bitcast(I32), y_codes[:].bitcast(I32))
+
+        empty_banks(0)
+        round_y(0)
+        empty_banks(1)
+        quantise_y(0)
+        round_y(1)
+        quantise_y(1)
         for q in range(4):
-            queue = nc.sync if q % 2 == 0 else nc.scalar
-            queue.dma_start(
+            nc.scalar.dma_start(
                 out_2[:, 4 * q : 4 * q + 4, :].rearrange("g r m -> r g m").bitcast(I32),
                 y_planes[32 * q : 32 * q + 4, :, :].bitcast(I32),
             )

@@ -25,6 +25,7 @@ R_PASSES = H // PASS
 N_GROUPS = N // PASS
 HALF = S // 2
 LABEL_BUFS = 8
+BIAS_ROW, WEIGHT_ROW = 16, 20
 
 
 def tile_list_click_feature_grad_kernel(
@@ -48,8 +49,8 @@ def tile_list_click_feature_grad_kernel(
         nc.gpsimd.memset(wb_scale_rows[:].bitcast(I32), 0)
         make_identity(nc, identity[:])
 
-        nc.scalar.dma_start(slot_rows[0:R_PASSES, :], b.rearrange("(a r) -> a r", r=PASS))
-        nc.scalar.dma_start(slot_rows[R_PASSES : 2 * R_PASSES, :], c.rearrange("(a r) -> a r", r=PASS))
+        nc.scalar.dma_start(slot_rows[BIAS_ROW : BIAS_ROW + R_PASSES, :], b.rearrange("(a r) -> a r", r=PASS))
+        nc.scalar.dma_start(slot_rows[WEIGHT_ROW : WEIGHT_ROW + R_PASSES, :], c.rearrange("(a r) -> a r", r=PASS))
         for q in range(4):
             nc.scalar.dma_start(
                 tab_scale_rows[32 * q + 4 : 32 * q + 4 + 4 * K_PASSES, :].bitcast(I32),
@@ -93,8 +94,8 @@ def tile_list_click_feature_grad_kernel(
             nc.tensor.transpose(turned[:, t, :], slot_rows[:, t::PACK], identity[:])
         bias = keep.tile([P, PACK, R_PASSES], F32, name="bias")
         minus_weight = keep.tile([P, PACK, R_PASSES], F32, name="minus_weight")
-        nc.scalar.copy(bias[:], turned[:, :, 0:R_PASSES])
-        nc.scalar.activation(minus_weight[:], turned[:, :, R_PASSES : 2 * R_PASSES], ACT.Copy, scale=-1.0)
+        nc.scalar.copy(bias[:], turned[:, :, BIAS_ROW : BIAS_ROW + R_PASSES])
+        nc.scalar.activation(minus_weight[:], turned[:, :, WEIGHT_ROW : WEIGHT_ROW + R_PASSES], ACT.Copy, scale=-1.0)
 
         a_round, a_codes, a_planes, prob = {}, {}, {}, {}
 
@@ -154,15 +155,18 @@ def tile_list_click_feature_grad_kernel(
         def logit_gradient(rp, t):
             scale = minus_weight[:, t, rp : rp + 1]
             window = label_rows[rp, t][:]
-            if rp == last and t >= 2:
-                first = ring.tile([P, HALF], F32, name="miss_first")
-                second = ring.tile([P, HALF], F32, name="miss_second")
+            if rp == last and t == PACK - 1:
+                first = ring.tile([P, HALF], F32, name="miss_first", bufs=1)
+                second = ring.tile([P, HALF], F32, name="miss_second", tag="miss_shared", bufs=1)
                 nc.vector.tensor_tensor(first[:], window.indirect(offsets[:, : HALF // 16]), prob[rp, t][:, :HALF], ALU.subtract)
                 nc.vector.tensor_tensor(second[:], window.indirect(offsets[:, HALF // 16 :]), prob[rp, t][:, HALF:], ALU.subtract)
                 nc.scalar.activation(d_round[rp][:, :HALF, t], first[:], ACT.Copy, scale=scale)
                 nc.vector.tensor_scalar(d_round[rp][:, HALF:, t], second[:], scale, None, ALU.mult)
             else:
-                miss = ring.tile([P, S], F32, name="miss", bufs=3)
+                if rp == last and t == PACK - 2:
+                    miss = ring.tile([P, S], F32, name="miss", tag="miss_shared", bufs=1)
+                else:
+                    miss = ring.tile([P, S], F32, name="miss", bufs=3)
                 nc.vector.tensor_tensor(miss[:], window.indirect(offsets[:]), prob[rp, t][:], ALU.subtract)
                 if rp == 0 and t < 2:
                     nc.vector.tensor_scalar(d_round[rp][:, :, t], miss[:], scale, None, ALU.mult)
@@ -202,33 +206,44 @@ def tile_list_click_feature_grad_kernel(
             rows = out_0[g * PASS : (g + 1) * PASS, :].rearrange("(p t) j -> p t j", t=PACK)
             for t in range(PACK):
                 bank = y_banks[g * PACK + t]
-                if (g == 0 and t % 2 == 1) or (g == 1 and t == 3):
+                if g == 0 and t == 0:
+                    for cols in (slice(0, HALF), slice(HALF, S)):
+                        nc.scalar.copy(y[g][:, t, cols], bank[:, cols])
+                        nc.sync.dma_start(rows[:, t, cols], y[g][:, t, cols])
+                elif t == 1 or (g == 0 and t == 3):
                     nc.vector.tensor_copy(y[g][:, t, :], bank[:])
                 else:
                     nc.scalar.copy(y[g][:, t, :], bank[:])
-                if g == 0 and t < 2:
+                if g == 0 and t == 1:
                     nc.sync.dma_start(rows[:, t, :], y[g][:, t, :])
                 elif t % 2 == 1:
                     nc.sync.dma_start(rows[:, t - 1 : t + 1, :], y[g][:, t - 1 : t + 1, :])
 
         def round_y(g):
-            y_round.append(ring.tile([P, PACK * S], BF16, name="y_round", tag="round", align_bytes=64))
+            y_round.append(ring.tile([P, S, PACK], BF16, name="y_round", tag="round", align_bytes=64))
+            split = S if g == 0 else HALF
             nc.vector.tensor_copy(
-                y_round[g][:].rearrange("p (u i t) -> p u t i", i=4, t=PACK),
-                y[g][:].rearrange("p t (u i) -> p u t i", i=4),
+                y_round[g][:, :split, :].rearrange("p (u i) t -> p u t i", i=4),
+                y[g][:, :, :split].rearrange("p t (u i) -> p u t i", i=4),
             )
+            if split < S:
+                nc.scalar.copy(
+                    y_round[g][:, split:, :].rearrange("p (u i) t -> p u t i", i=4),
+                    y[g][:, :, split:].rearrange("p t (u i) -> p u t i", i=4),
+                )
 
         def quantise_y(g):
             y_codes = keep.tile([P, S], U32, name="y_codes%d" % g, align_bytes=64)
-            nc.vector.quantize_mx(y_codes[:].bitcast(FP8X4), y_planes[:, g, :], y_round[g][:])
-            nc.sync.dma_start(out_1[g].rearrange("p m t -> p (m t)").bitcast(I32), y_codes[:].bitcast(I32))
+            words = out_1[g].rearrange("p m t -> p (m t)").bitcast(I32)
+            for cols in [slice(0, S)] if g == 0 else [slice(0, HALF), slice(HALF, S)]:
+                nc.vector.quantize_mx(
+                    y_codes[:, cols].bitcast(FP8X4), y_planes[:, g, cols], y_round[g][:, cols, :].rearrange("p s t -> p (s t)")
+                )
+                nc.sync.dma_start(words[:, cols], y_codes[:, cols].bitcast(I32))
 
-        empty_banks(0)
-        round_y(0)
-        empty_banks(1)
-        quantise_y(0)
-        round_y(1)
-        quantise_y(1)
+        for stage in (empty_banks, round_y, quantise_y):
+            for g in range(N_GROUPS):
+                stage(g)
         for q in range(4):
             nc.scalar.dma_start(
                 out_2[:, 4 * q : 4 * q + 4, :].rearrange("g r m -> r g m").bitcast(I32),

@@ -25,7 +25,7 @@ R_PASSES = H // PASS
 N_GROUPS = N // PASS
 HALF = S // 2
 LABEL_BUFS = 8
-BIAS_ROW, WEIGHT_ROW = 16, 20
+BIAS_ROWS, WEIGHT_ROWS = slice(12, 24, 4), slice(76, 88, 4)
 
 
 def tile_list_click_feature_grad_kernel(
@@ -45,21 +45,21 @@ def tile_list_click_feature_grad_kernel(
         slot_rows = keep.tile([P, PASS], F32, name="slot_rows")
         identity = keep.tile([P, P], F32, name="identity")
         nc.gpsimd.memset(slot_rows[:], 0.0)
-        nc.vector.memset(tab_scale_rows[:].bitcast(I32), 0)
-        nc.gpsimd.memset(wb_scale_rows[:].bitcast(I32), 0)
         make_identity(nc, identity[:])
+        nc.vector.memset(tab_scale_rows[:].bitcast(I32), 0)
+        nc.vector.memset(wb_scale_rows[:].bitcast(I32), 0)
 
-        nc.scalar.dma_start(slot_rows[BIAS_ROW : BIAS_ROW + R_PASSES, :], b.rearrange("(a r) -> a r", r=PASS))
-        nc.scalar.dma_start(slot_rows[WEIGHT_ROW : WEIGHT_ROW + R_PASSES, :], c.rearrange("(a r) -> a r", r=PASS))
+        nc.scalar.dma_start(slot_rows[BIAS_ROWS, :], b.rearrange("(a r) -> a r", r=PASS))
+        nc.scalar.dma_start(slot_rows[WEIGHT_ROWS, :], c.rearrange("(a r) -> a r", r=PASS))
         for q in range(4):
-            nc.scalar.dma_start(
+            nc.gpsimd.dma_start(
                 tab_scale_rows[32 * q + 4 : 32 * q + 4 + 4 * K_PASSES, :].bitcast(I32),
                 tab_scales[:, 4 * q : 4 * q + 4, :].bitcast(I32),
             )
-        for q in range(4):
-            nc.scalar.dma_start(
-                wb_scale_rows[32 * q : 32 * q + 4, :, :].bitcast(I32),
-                wb_scales[:, 4 * q : 4 * q + 4, :].rearrange("a r n -> r a n").bitcast(I32),
+        for r in range(4):
+            nc.gpsimd.dma_start(
+                wb_scale_rows[r:P:32, :, :].bitcast(I32),
+                wb_scales[:, r::4, :].rearrange("a q n -> q a n").bitcast(I32),
             )
 
         wb_raw = keep.tile([P, R_PASSES, 2 * N], U8, name="wb_raw", align_bytes=64)
@@ -94,8 +94,8 @@ def tile_list_click_feature_grad_kernel(
             nc.tensor.transpose(turned[:, t, :], slot_rows[:, t::PACK], identity[:])
         bias = keep.tile([P, PACK, R_PASSES], F32, name="bias")
         minus_weight = keep.tile([P, PACK, R_PASSES], F32, name="minus_weight")
-        nc.scalar.copy(bias[:], turned[:, :, BIAS_ROW : BIAS_ROW + R_PASSES])
-        nc.scalar.activation(minus_weight[:], turned[:, :, WEIGHT_ROW : WEIGHT_ROW + R_PASSES], ACT.Copy, scale=-1.0)
+        nc.scalar.copy(bias[:], turned[:, :, BIAS_ROWS])
+        nc.scalar.activation(minus_weight[:], turned[:, :, WEIGHT_ROWS], ACT.Copy, scale=-1.0)
 
         a_round, a_codes, a_planes, prob = {}, {}, {}, {}
 
@@ -103,8 +103,8 @@ def tile_list_click_feature_grad_kernel(
             a_round[kp, rp] = ring.tile([P, PACK * PASS], BF16, name="a_round", tag="round", align_bytes=64)
             dealt = a_round[kp, rp][:].rearrange("p (u e m j) -> p u m j e", u=2, e=2, j=PACK)
             block = a_raw[kp][:, :, rp * PASS : (rp + 1) * PASS].rearrange("p j (m u e) -> p u m j e", u=2, e=2)
-            for u in range(2):
-                nc.vector.tensor_copy(dealt[:, u], block[:, u])
+            nc.vector.tensor_copy(dealt[:, 0], block[:, 0])
+            nc.scalar.copy(dealt[:, 1], block[:, 1])
 
         def quantise_a(kp, rp):
             a_codes[kp, rp] = keep.tile([P, PASS], U32, name="a_codes%d%d" % (kp, rp), align_bytes=64)

@@ -20,11 +20,19 @@ ACT = mybir.ActivationFunctionType
 P = 128
 PACK = 4
 PASS = P * PACK
+QUADS = 4
+QUAD_ROWS = 4
 K_PASSES = K // PASS
 R_PASSES = H // PASS
 N_GROUPS = N // PASS
+LAST = R_PASSES - 1
 HALF = S // 2
+HALVES = (slice(0, HALF), slice(HALF, S))
+WHOLE = (slice(0, S),)
+NEAR = 4
+PSUM_BANKS = 8
 LABEL_BUFS = 8
+MISS_BUFS = 3
 BIAS_ROWS, WEIGHT_ROWS = slice(12, 24, 4), slice(76, 88, 4)
 
 
@@ -35,7 +43,7 @@ def tile_list_click_feature_grad_kernel(
     with ExitStack() as ctx:
         keep = ctx.enter_context(tc.tile_pool(name="keep", bufs=1))
         ring = ctx.enter_context(tc.tile_pool(name="ring", bufs=2))
-        psum = ctx.enter_context(tc.psum_pool(name="psum", bufs=8))
+        psum = ctx.enter_context(tc.psum_pool(name="psum", bufs=PSUM_BANKS))
 
         offsets = keep.tile([P, S // 16], U16, name="offsets")
         nc.sync.dma_start(offsets[:], offs)
@@ -49,30 +57,34 @@ def tile_list_click_feature_grad_kernel(
         nc.vector.memset(tab_scale_rows[:].bitcast(I32), 0)
         nc.vector.memset(wb_scale_rows[:].bitcast(I32), 0)
 
-        nc.scalar.dma_start(slot_rows[BIAS_ROWS, :], b.rearrange("(a r) -> a r", r=PASS))
-        nc.scalar.dma_start(slot_rows[WEIGHT_ROWS, :], c.rearrange("(a r) -> a r", r=PASS))
-        for q in range(4):
+        nc.scalar.dma_start(slot_rows[BIAS_ROWS, :], b.rearrange("(rp r) -> rp r", r=PASS))
+        nc.scalar.dma_start(slot_rows[WEIGHT_ROWS, :], c.rearrange("(rp r) -> rp r", r=PASS))
+        for quad in range(QUADS):
             nc.gpsimd.dma_start(
-                tab_scale_rows[32 * q + 4 : 32 * q + 4 + 4 * K_PASSES, :].bitcast(I32),
-                tab_scales[:, 4 * q : 4 * q + 4, :].bitcast(I32),
+                tab_scale_rows[32 * quad + QUAD_ROWS : 32 * quad + QUAD_ROWS * (1 + K_PASSES), :].bitcast(I32),
+                tab_scales[:, QUAD_ROWS * quad : QUAD_ROWS * (quad + 1), :].bitcast(I32),
             )
-        for r in range(4):
-            nc.gpsimd.dma_start(
-                wb_scale_rows[r:P:32, :, :].bitcast(I32),
-                wb_scales[:, r::4, :].rearrange("a q n -> q a n").bitcast(I32),
+        for row in range(QUAD_ROWS):
+            nc.scalar.dma_start(
+                wb_scale_rows[row:P:32, :, :].bitcast(I32),
+                wb_scales[:, row::QUAD_ROWS, :].rearrange("rp quad n -> quad rp n").bitcast(I32),
             )
 
         wb_raw = keep.tile([P, R_PASSES, 2 * N], U8, name="wb_raw", align_bytes=64)
-        nc.sync.dma_start(wb_raw[:].bitcast(I32), wb_words.rearrange("a p e -> p a e").bitcast(I32))
+        nc.sync.dma_start(wb_raw[:].bitcast(I32), wb_words.rearrange("rp p w -> p rp w").bitcast(I32))
         a_raw = [ring.tile([P, PACK, H], F32, name="a_raw", tag="wide") for kp in range(K_PASSES)]
         tab = [keep.tile([P, T], I32, name="tab%d" % kp, align_bytes=64) for kp in range(K_PASSES)]
-        a_rows = a.rearrange("(k p j) r -> k p j r", p=P, j=PACK)
+        a_rows = a.rearrange("(kp p i) r -> kp p i r", p=P, i=PACK)
         nc.sync.dma_start(a_raw[0][:], a_rows[0])
         for kp in range(K_PASSES):
-            nc.sync.dma_start(tab[kp][:], tab_words[kp].rearrange("p t i -> p (t i)").bitcast(I32))
+            nc.sync.dma_start(tab[kp][:], tab_words[kp].rearrange("p x i -> p (x i)").bitcast(I32))
         nc.sync.dma_start(a_raw[1][:], a_rows[1])
 
-        order = [(0, 0), (0, 1), (0, 2), (1, 0), (1, 1), (1, 2), (2, 0), (0, 3), (2, 1), (1, 3), (2, 2), (2, 3)]
+        order = [(rp, t) for rp in range(LAST) for t in range(PACK - 1)]
+        for t in range(PACK):
+            order.append((LAST, t))
+            if t < LAST:
+                order.append((t, PACK - 1))
         label_rows = {}
 
         def load_labels(rp, t):
@@ -85,8 +97,8 @@ def tile_list_click_feature_grad_kernel(
 
         wb_codes = keep.tile([P, R_PASSES, 2 * N], U8, name="wb_codes", align_bytes=64)
         nc.vector.tensor_copy(
-            wb_codes[:].bitcast(U16).rearrange("p a (g t m) -> p (a g) t m", g=N_GROUPS, t=PACK),
-            wb_raw[:].bitcast(U16).rearrange("p a (g m t) -> p (a g) t m", g=N_GROUPS, t=PACK),
+            wb_codes[:].bitcast(U16).rearrange("p rp (g t m) -> p (rp g) t m", g=N_GROUPS, t=PACK),
+            wb_raw[:].bitcast(U16).rearrange("p rp (g m t) -> p (rp g) t m", g=N_GROUPS, t=PACK),
         )
 
         turned = psum.tile([P, PACK, P], F32, name="bank")
@@ -101,10 +113,10 @@ def tile_list_click_feature_grad_kernel(
 
         def round_a(kp, rp):
             a_round[kp, rp] = ring.tile([P, PACK * PASS], BF16, name="a_round", tag="round", align_bytes=64)
-            dealt = a_round[kp, rp][:].rearrange("p (u e m j) -> p u m j e", u=2, e=2, j=PACK)
-            block = a_raw[kp][:, :, rp * PASS : (rp + 1) * PASS].rearrange("p j (m u e) -> p u m j e", u=2, e=2)
-            nc.vector.tensor_copy(dealt[:, 0], block[:, 0])
-            nc.scalar.copy(dealt[:, 1], block[:, 1])
+            dealt = a_round[kp, rp][:].rearrange("p (u e m i) -> p u m i e", u=2, e=2, i=PACK)
+            block = a_raw[kp][:, :, rp * PASS : (rp + 1) * PASS].rearrange("p i (m u e) -> p u m i e", u=2, e=2)
+            for u in range(2):
+                nc.vector.tensor_copy(dealt[:, u], block[:, u])
 
         def quantise_a(kp, rp):
             a_codes[kp, rp] = keep.tile([P, PASS], U32, name="a_codes%d%d" % (kp, rp), align_bytes=64)
@@ -114,11 +126,12 @@ def tile_list_click_feature_grad_kernel(
         def prepare_a(kp):
             round_a(kp, 0)
             for rp in range(R_PASSES):
-                if rp + 1 < R_PASSES:
+                if rp < LAST:
                     round_a(kp, rp + 1)
                 quantise_a(kp, rp)
 
         prepare_a(0)
+
         v_codes = [keep.tile([P, S], U32, name="v_codes%d" % kp, align_bytes=64) for kp in range(K_PASSES)]
         for kp in range(K_PASSES):
             nc.vector.tensor_copy(v_codes[kp][:], tab[kp][:].bitcast(U32).indirect(offsets[:]))
@@ -126,9 +139,10 @@ def tile_list_click_feature_grad_kernel(
         nc.vector.tensor_copy(v_planes[:], tab_scale_rows[:].indirect(offsets[:]))
         wb_planes = keep.tile([P, R_PASSES, N], U8, name="wb_planes", tag="tab1", align_bytes=64)
         nc.vector.tensor_copy(
-            wb_planes[:].rearrange("p a (g t m) -> p (a g) t m", g=N_GROUPS, t=PACK),
-            wb_scale_rows[:].rearrange("p a (g m t) -> p (a g) t m", g=N_GROUPS, t=PACK),
+            wb_planes[:].rearrange("p rp (g t m) -> p (rp g) t m", g=N_GROUPS, t=PACK),
+            wb_scale_rows[:].rearrange("p rp (g m t) -> p (rp g) t m", g=N_GROUPS, t=PACK),
         )
+
         prepare_a(1)
 
         for rp in range(R_PASSES):
@@ -141,7 +155,7 @@ def tile_list_click_feature_grad_kernel(
                         lhsT=a_codes[kp, rp][:, cols].bitcast(FP8X4),
                         lhsT_scale=a_planes[kp, rp][:, cols],
                         rhs=v_codes[kp][:].bitcast(FP8X4),
-                        rhs_scale=v_planes[4 * kp + 4 : P, :],
+                        rhs_scale=v_planes[QUAD_ROWS * (1 + kp) : P, :],
                         start=(kp == 0),
                         stop=(kp == K_PASSES - 1),
                     )
@@ -149,24 +163,27 @@ def tile_list_click_feature_grad_kernel(
                 nc.scalar.activation(prob[rp, t][:], logits[:], ACT.Sigmoid, bias=bias[:, t, rp : rp + 1])
 
         d_round = [keep.tile([P, S, PACK], BF16, name="d_round%d" % rp, align_bytes=64) for rp in range(R_PASSES)]
-        y_banks = [psum.tile([P, S], F32, name="bank") for i in range(N_GROUPS * PACK)]
-        last = R_PASSES - 1
+        y_banks = [psum.tile([P, S], F32, name="bank") for bank_no in range(N_GROUPS * PACK)]
 
         def logit_gradient(rp, t):
             scale = minus_weight[:, t, rp : rp + 1]
             window = label_rows[rp, t][:]
-            if rp == last and t == PACK - 1:
+            if rp == LAST and t == PACK - 1:
                 first = ring.tile([P, HALF], F32, name="miss_first", bufs=1)
                 second = ring.tile([P, HALF], F32, name="miss_second", tag="miss_shared", bufs=1)
-                nc.vector.tensor_tensor(first[:], window.indirect(offsets[:, : HALF // 16]), prob[rp, t][:, :HALF], ALU.subtract)
-                nc.vector.tensor_tensor(second[:], window.indirect(offsets[:, HALF // 16 :]), prob[rp, t][:, HALF:], ALU.subtract)
+                nc.vector.tensor_tensor(
+                    first[:], window.indirect(offsets[:, : HALF // 16]), prob[rp, t][:, :HALF], ALU.subtract
+                )
+                nc.vector.tensor_tensor(
+                    second[:], window.indirect(offsets[:, HALF // 16 :]), prob[rp, t][:, HALF:], ALU.subtract
+                )
                 nc.scalar.activation(d_round[rp][:, :HALF, t], first[:], ACT.Copy, scale=scale)
                 nc.vector.tensor_scalar(d_round[rp][:, HALF:, t], second[:], scale, None, ALU.mult)
             else:
-                if rp == last and t == PACK - 2:
+                if rp == LAST and t == PACK - 2:
                     miss = ring.tile([P, S], F32, name="miss", tag="miss_shared", bufs=1)
                 else:
-                    miss = ring.tile([P, S], F32, name="miss", bufs=3)
+                    miss = ring.tile([P, S], F32, name="miss", bufs=MISS_BUFS)
                 nc.vector.tensor_tensor(miss[:], window.indirect(offsets[:]), prob[rp, t][:], ALU.subtract)
                 if rp == 0 and t < 2:
                     nc.vector.tensor_scalar(d_round[rp][:, :, t], miss[:], scale, None, ALU.mult)
@@ -174,28 +191,30 @@ def tile_list_click_feature_grad_kernel(
                     nc.scalar.activation(d_round[rp][:, :, t], miss[:], ACT.Copy, scale=scale)
 
         def back_project(rp):
-            d_codes = keep.tile([P, S], U32, name="d_codes", tag="prob%d%d" % (last, rp + 1), align_bytes=64)
+            d_codes = keep.tile([P, S], U32, name="d_codes", tag="prob%d%d" % (LAST, rp + 1), align_bytes=64)
             d_plane = keep.tile([P, S], U8, name="d_plane%d" % rp, align_bytes=64)
-            for cols in [slice(0, HALF), slice(HALF, S)] if rp == last else [slice(0, S)]:
+            for cols in HALVES if rp == LAST else WHOLE:
                 nc.vector.quantize_mx(
-                    d_codes[:, cols].bitcast(FP8X4), d_plane[:, cols], d_round[rp][:, cols, :].rearrange("p s t -> p (s t)")
+                    d_codes[:, cols].bitcast(FP8X4),
+                    d_plane[:, cols],
+                    d_round[rp][:, cols, :].rearrange("p j t -> p (j t)"),
                 )
-            for i in range(N_GROUPS * PACK):
+            for bank_no in range(N_GROUPS * PACK):
                 nc.tensor.matmul_mx(
-                    y_banks[i][:],
-                    lhsT=wb_codes[:, rp, 2 * P * i : 2 * P * (i + 1)].bitcast(FP4X4),
-                    lhsT_scale=wb_planes[:, rp, P * i : P * (i + 1)],
+                    y_banks[bank_no][:],
+                    lhsT=wb_codes[:, rp, 2 * P * bank_no : 2 * P * (bank_no + 1)].bitcast(FP4X4),
+                    lhsT_scale=wb_planes[:, rp, P * bank_no : P * (bank_no + 1)],
                     rhs=d_codes[:].bitcast(FP8X4),
                     rhs_scale=d_plane[:],
                     start=(rp == 0),
-                    stop=(rp == last),
+                    stop=(rp == LAST),
                 )
 
         for step, (rp, t) in enumerate(order):
             logit_gradient(rp, t)
             if step + LABEL_BUFS < len(order):
                 load_labels(*order[step + LABEL_BUFS])
-            if rp == last and t >= 1:
+            if rp == LAST and t >= 1:
                 back_project(t - 1)
 
         y_planes = keep.tile([P, N_GROUPS, S], U8, name="y_planes", align_bytes=64)
@@ -207,7 +226,7 @@ def tile_list_click_feature_grad_kernel(
             for t in range(PACK):
                 bank = y_banks[g * PACK + t]
                 if g == 0 and t == 0:
-                    for cols in (slice(0, HALF), slice(HALF, S)):
+                    for cols in HALVES:
                         nc.scalar.copy(y[g][:, t, cols], bank[:, cols])
                         nc.sync.dma_start(rows[:, t, cols], y[g][:, t, cols])
                 elif t == 1 or (g == 0 and t == 3):
@@ -223,29 +242,31 @@ def tile_list_click_feature_grad_kernel(
             y_round.append(ring.tile([P, S, PACK], BF16, name="y_round", tag="round", align_bytes=64))
             split = S if g == 0 else HALF
             nc.vector.tensor_copy(
-                y_round[g][:, :split, :].rearrange("p (u i) t -> p u t i", i=4),
-                y[g][:, :, :split].rearrange("p t (u i) -> p u t i", i=4),
+                y_round[g][:, :split, :].rearrange("p (run near) t -> p run t near", near=NEAR),
+                y[g][:, :, :split].rearrange("p t (run near) -> p run t near", near=NEAR),
             )
             if split < S:
                 nc.scalar.copy(
-                    y_round[g][:, split:, :].rearrange("p (u i) t -> p u t i", i=4),
-                    y[g][:, :, split:].rearrange("p t (u i) -> p u t i", i=4),
+                    y_round[g][:, split:, :].rearrange("p (run near) t -> p run t near", near=NEAR),
+                    y[g][:, :, split:].rearrange("p t (run near) -> p run t near", near=NEAR),
                 )
 
         def quantise_y(g):
             y_codes = keep.tile([P, S], U32, name="y_codes%d" % g, align_bytes=64)
-            words = out_1[g].rearrange("p m t -> p (m t)").bitcast(I32)
-            for cols in [slice(0, S)] if g == 0 else [slice(0, HALF), slice(HALF, S)]:
+            words = out_1[g].rearrange("p j t -> p (j t)").bitcast(I32)
+            for cols in WHOLE if g == 0 else HALVES:
                 nc.vector.quantize_mx(
-                    y_codes[:, cols].bitcast(FP8X4), y_planes[:, g, cols], y_round[g][:, cols, :].rearrange("p s t -> p (s t)")
+                    y_codes[:, cols].bitcast(FP8X4),
+                    y_planes[:, g, cols],
+                    y_round[g][:, cols, :].rearrange("p j t -> p (j t)"),
                 )
                 nc.sync.dma_start(words[:, cols], y_codes[:, cols].bitcast(I32))
 
         for stage in (empty_banks, round_y, quantise_y):
             for g in range(N_GROUPS):
                 stage(g)
-        for q in range(4):
+        for quad in range(QUADS):
             nc.scalar.dma_start(
-                out_2[:, 4 * q : 4 * q + 4, :].rearrange("g r m -> r g m").bitcast(I32),
-                y_planes[32 * q : 32 * q + 4, :, :].bitcast(I32),
+                out_2[:, QUAD_ROWS * quad : QUAD_ROWS * (quad + 1), :].rearrange("g row j -> row g j").bitcast(I32),
+                y_planes[32 * quad : 32 * quad + QUAD_ROWS, :, :].bitcast(I32),
             )

@@ -32,6 +32,7 @@ WHOLE = (slice(0, S),)
 NEAR = 4
 PSUM_BANKS = 8
 LABEL_BUFS = 8
+ROUND_BUFS = R_PASSES
 MISS_BUFS = 3
 BIAS_ROWS, WEIGHT_ROWS = slice(12, 24, 4), slice(76, 88, 4)
 
@@ -106,17 +107,22 @@ def tile_list_click_feature_grad_kernel(
             nc.tensor.transpose(turned[:, t, :], slot_rows[:, t::PACK], identity[:])
         bias = keep.tile([P, PACK, R_PASSES], F32, name="bias")
         minus_weight = keep.tile([P, PACK, R_PASSES], F32, name="minus_weight")
+        warm = keep.tile([P, 1], F32, name="warm")
+        nc.scalar.activation(warm[:], turned[:, 0, 0:1], ACT.Sigmoid)
         nc.scalar.copy(bias[:], turned[:, :, BIAS_ROWS])
         nc.scalar.activation(minus_weight[:], turned[:, :, WEIGHT_ROWS], ACT.Copy, scale=-1.0)
 
         a_round, a_codes, a_planes, prob = {}, {}, {}, {}
 
         def round_a(kp, rp):
-            a_round[kp, rp] = ring.tile([P, PACK * PASS], BF16, name="a_round", tag="round", align_bytes=64)
+            a_round[kp, rp] = ring.tile([P, PACK * PASS], BF16, name="a_round", tag="round", bufs=ROUND_BUFS, align_bytes=64)
             dealt = a_round[kp, rp][:].rearrange("p (u e m i) -> p u m i e", u=2, e=2, i=PACK)
             block = a_raw[kp][:, :, rp * PASS : (rp + 1) * PASS].rearrange("p i (m u e) -> p u m i e", u=2, e=2)
             for u in range(2):
-                nc.vector.tensor_copy(dealt[:, u], block[:, u])
+                if rp == LAST:
+                    nc.scalar.copy(dealt[:, u], block[:, u])
+                else:
+                    nc.vector.tensor_copy(dealt[:, u], block[:, u])
 
         def quantise_a(kp, rp):
             a_codes[kp, rp] = keep.tile([P, PASS], U32, name="a_codes%d%d" % (kp, rp), align_bytes=64)
@@ -124,10 +130,9 @@ def tile_list_click_feature_grad_kernel(
             nc.vector.quantize_mx(a_codes[kp, rp][:].bitcast(FP8X4), a_planes[kp, rp][:], a_round[kp, rp][:])
 
         def prepare_a(kp):
-            round_a(kp, 0)
             for rp in range(R_PASSES):
-                if rp < LAST:
-                    round_a(kp, rp + 1)
+                round_a(kp, rp)
+            for rp in range(R_PASSES):
                 quantise_a(kp, rp)
 
         prepare_a(0)
@@ -239,7 +244,7 @@ def tile_list_click_feature_grad_kernel(
                     nc.sync.dma_start(rows[:, t - 1 : t + 1, :], y[g][:, t - 1 : t + 1, :])
 
         def round_y(g):
-            y_round.append(ring.tile([P, S, PACK], BF16, name="y_round", tag="round", align_bytes=64))
+            y_round.append(ring.tile([P, S, PACK], BF16, name="y_round", tag="round", bufs=ROUND_BUFS, align_bytes=64))
             split = S if g == 0 else HALF
             nc.vector.tensor_copy(
                 y_round[g][:, :split, :].rearrange("p (run near) t -> p run t near", near=NEAR),

@@ -28,6 +28,7 @@ N_GROUPS = N // PASS
 LAST = R_PASSES - 1
 HALF = S // 2
 HALVES = (slice(0, HALF), slice(HALF, S))
+QUARTERS = tuple(slice(q * S // 4, (q + 1) * S // 4) for q in range(4))
 WHOLE = (slice(0, S),)
 NEAR = 4
 PSUM_BANKS = 8
@@ -172,33 +173,21 @@ def tile_list_click_feature_grad_kernel(
 
         def logit_gradient(rp, t):
             scale = minus_weight[:, t, rp : rp + 1]
-            window = label_rows[rp, t][:]
-            if rp == LAST and t == PACK - 1:
-                first = ring.tile([P, HALF], F32, name="miss_first", bufs=1)
-                second = ring.tile([P, HALF], F32, name="miss_second", tag="miss_shared", bufs=1)
-                nc.vector.tensor_tensor(
-                    first[:], window.indirect(offsets[:, : HALF // 16]), prob[rp, t][:, :HALF], ALU.subtract
-                )
-                nc.vector.tensor_tensor(
-                    second[:], window.indirect(offsets[:, HALF // 16 :]), prob[rp, t][:, HALF:], ALU.subtract
-                )
-                nc.scalar.activation(d_round[rp][:, :HALF, t], first[:], ACT.Copy, scale=scale)
-                nc.vector.tensor_scalar(d_round[rp][:, HALF:, t], second[:], scale, None, ALU.mult)
-            else:
-                if rp == LAST and t == PACK - 2:
-                    miss = ring.tile([P, S], F32, name="miss", tag="miss_shared", bufs=1)
-                else:
-                    miss = ring.tile([P, S], F32, name="miss", bufs=MISS_BUFS)
-                nc.vector.tensor_tensor(miss[:], window.indirect(offsets[:]), prob[rp, t][:], ALU.subtract)
+            miss = ring.tile([P, S], F32, name="miss", bufs=MISS_BUFS)
+            pieces = {(LAST, PACK - 1): QUARTERS, (LAST, PACK - 2): HALVES}.get((rp, t), WHOLE)
+            for cols in pieces:
+                picked = label_rows[rp, t][:].indirect(offsets[:, cols.start // 16 : cols.stop // 16])
+                nc.vector.tensor_tensor(miss[:, cols], picked, prob[rp, t][:, cols], ALU.subtract)
+            for cols in pieces:
                 if rp == 0 and t < 2:
-                    nc.vector.tensor_scalar(d_round[rp][:, :, t], miss[:], scale, None, ALU.mult)
+                    nc.vector.tensor_scalar(d_round[rp][:, cols, t], miss[:, cols], scale, None, ALU.mult)
                 else:
-                    nc.scalar.activation(d_round[rp][:, :, t], miss[:], ACT.Copy, scale=scale)
+                    nc.scalar.activation(d_round[rp][:, cols, t], miss[:, cols], ACT.Copy, scale=scale)
 
         def back_project(rp):
             d_codes = keep.tile([P, S], U32, name="d_codes", tag="prob%d%d" % (LAST, rp + 1), align_bytes=64)
             d_plane = keep.tile([P, S], U8, name="d_plane%d" % rp, align_bytes=64)
-            for cols in HALVES if rp == LAST else WHOLE:
+            for cols in (HALVES[0],) + QUARTERS[2:] if rp == LAST else WHOLE:
                 nc.vector.quantize_mx(
                     d_codes[:, cols].bitcast(FP8X4),
                     d_plane[:, cols],

@@ -184,32 +184,51 @@ def tile_list_click_feature_grad_kernel(
                 else:
                     nc.scalar.activation(d_round[rp][:, cols, t], miss[:, cols], ACT.Copy, scale=scale)
 
-        def back_project(rp):
-            d_codes = keep.tile([P, S], U32, name="d_codes", tag="prob%d%d" % (LAST, rp + 1), align_bytes=64)
-            d_plane = keep.tile([P, S], U8, name="d_plane%d" % rp, align_bytes=64)
+        d_codes, d_plane = {}, {}
+
+        def quantise_d(rp, after):
+            d_codes[rp] = keep.tile([P, S], U32, name="d_codes", tag="prob%d%d" % after, align_bytes=64)
+            d_plane[rp] = keep.tile([P, S], U8, name="d_plane%d" % rp, align_bytes=64)
             for cols in (HALVES[0],) + QUARTERS[2:] if rp == LAST else WHOLE:
                 nc.vector.quantize_mx(
-                    d_codes[:, cols].bitcast(FP8X4),
-                    d_plane[:, cols],
+                    d_codes[rp][:, cols].bitcast(FP8X4),
+                    d_plane[rp][:, cols],
                     d_round[rp][:, cols, :].rearrange("p j t -> p (j t)"),
                 )
-            for bank_no in range(N_GROUPS * PACK):
+
+        def back_project(rp, first):
+            def one_pass(out, rows_no, cols, start, stop):
                 nc.tensor.matmul_mx(
-                    y_banks[bank_no][:],
-                    lhsT=wb_codes[:, rp, 2 * P * bank_no : 2 * P * (bank_no + 1)].bitcast(FP4X4),
-                    lhsT_scale=wb_planes[:, rp, P * bank_no : P * (bank_no + 1)],
-                    rhs=d_codes[:].bitcast(FP8X4),
-                    rhs_scale=d_plane[:],
-                    start=(rp == 0),
-                    stop=(rp == LAST),
+                    out,
+                    lhsT=wb_codes[:, rp, 2 * P * rows_no : 2 * P * (rows_no + 1)].bitcast(FP4X4),
+                    lhsT_scale=wb_planes[:, rp, P * rows_no : P * (rows_no + 1)],
+                    rhs=d_codes[rp][:, cols].bitcast(FP8X4),
+                    rhs_scale=d_plane[rp][:, cols],
+                    start=start,
+                    stop=stop,
                 )
+
+            for half in range(2):
+                for q in range(2):
+                    for t in range(2):
+                        place = t * HALF + q * P
+                        one_pass(
+                            y_banks[half][:, place : place + P],
+                            t,
+                            QUARTERS[2 * half + q],
+                            first and q == 0 and t == 0,
+                            rp == LAST and q == 1 and t == 1,
+                        )
+            for bank_no in range(2, N_GROUPS * PACK):
+                one_pass(y_banks[bank_no][:], bank_no, WHOLE[0], first, rp == LAST)
 
         for step, (rp, t) in enumerate(order):
             logit_gradient(rp, t)
             if step + LABEL_BUFS < len(order):
                 load_labels(*order[step + LABEL_BUFS])
             if rp == LAST and t >= 1:
-                back_project(t - 1)
+                quantise_d(t - 1, (rp, t))
+                back_project(t - 1, t == 1)
 
         y_planes = keep.tile([P, N_GROUPS, S], U8, name="y_planes", align_bytes=64)
         y, y_round = [], []
@@ -219,17 +238,18 @@ def tile_list_click_feature_grad_kernel(
             rows = out_0[g * PASS : (g + 1) * PASS, :].rearrange("(p t) j -> p t j", t=PACK)
             for t in range(PACK):
                 bank = y_banks[g * PACK + t]
-                if g == 0 and t == 0:
-                    for cols in HALVES:
-                        nc.scalar.copy(y[g][:, t, cols], bank[:, cols])
-                        nc.sync.dma_start(rows[:, t, cols], y[g][:, t, cols])
+                if g == 0 and t < 2:
+                    for row in range(2):
+                        if t == 0:
+                            nc.scalar.copy(y[g][:, row, HALVES[t]], bank[:, HALVES[row]])
+                        else:
+                            nc.vector.tensor_copy(y[g][:, row, HALVES[t]], bank[:, HALVES[row]])
+                        nc.sync.dma_start(rows[:, row, HALVES[t]], y[g][:, row, HALVES[t]])
                 elif t == 1 or (g == 0 and t == 3):
                     nc.vector.tensor_copy(y[g][:, t, :], bank[:])
                 else:
                     nc.scalar.copy(y[g][:, t, :], bank[:])
-                if g == 0 and t == 1:
-                    nc.sync.dma_start(rows[:, t, :], y[g][:, t, :])
-                elif t % 2 == 1:
+                if t % 2 == 1 and (g, t) != (0, 1):
                     nc.sync.dma_start(rows[:, t - 1 : t + 1, :], y[g][:, t - 1 : t + 1, :])
 
         def round_y(g):

@@ -72,8 +72,8 @@ def tile_list_click_feature_grad_kernel(
                 wb_scales[:, row::QUAD_ROWS, :].rearrange("rp quad n -> quad rp n").bitcast(I32),
             )
 
-        wb_raw = keep.tile([P, R_PASSES, 2 * N], U8, name="wb_raw", align_bytes=64)
-        nc.sync.dma_start(wb_raw[:].bitcast(I32), wb_words.rearrange("rp p w -> p rp w").bitcast(I32))
+        wb_raw = keep.tile([P, LAST, 2 * N], U8, name="wb_raw", align_bytes=64)
+        nc.sync.dma_start(wb_raw[:].bitcast(I32), wb_words[:LAST].rearrange("rp p w -> p rp w").bitcast(I32))
         a_raw = [ring.tile([P, PACK, H], F32, name="a_raw", tag="wide") for kp in range(K_PASSES)]
         tab = [keep.tile([P, T], I32, name="tab%d" % kp, align_bytes=64) for kp in range(K_PASSES)]
         a_rows = a.rearrange("(kp p i) r -> kp p i r", p=P, i=PACK)
@@ -90,14 +90,14 @@ def tile_list_click_feature_grad_kernel(
         label_rows = {}
 
         def load_labels(rp, t):
-            label_rows[rp, t] = ring.tile([P, T], F32, name="label_rows", bufs=LABEL_BUFS)
+            label_rows[rp, t] = ring.tile([P, T], F32, name="label_rows", bufs=LABEL_BUFS, align_bytes=64)
             rows = gT[rp * PASS : (rp + 1) * PASS, :].rearrange("(p t) x -> p t x", t=PACK)
             nc.sync.dma_start(label_rows[rp, t][:], rows[:, t, :])
 
         for rp, t in order[:LABEL_BUFS]:
             load_labels(rp, t)
 
-        wb_codes = keep.tile([P, R_PASSES, 2 * N], U8, name="wb_codes", align_bytes=64)
+        wb_codes = keep.tile([P, LAST, 2 * N], U8, name="wb_codes", align_bytes=64)
         nc.vector.tensor_copy(
             wb_codes[:].bitcast(U16).rearrange("p rp (g t m) -> p (rp g) t m", g=N_GROUPS, t=PACK),
             wb_raw[:].bitcast(U16).rearrange("p rp (g m t) -> p (rp g) t m", g=N_GROUPS, t=PACK),
@@ -184,23 +184,43 @@ def tile_list_click_feature_grad_kernel(
                 else:
                     nc.scalar.activation(d_round[rp][:, cols, t], miss[:, cols], ACT.Copy, scale=scale)
 
-        d_codes, d_plane = {}, {}
+        d_codes, d_plane, last_codes, last_raw = {}, {}, {}, []
+
+        def load_last_words():
+            last_raw.append(ring.tile([P, 2 * N], U8, name="last_raw", tag="label_rows", bufs=LABEL_BUFS, align_bytes=64))
+            nc.sync.dma_start(last_raw[0][:].bitcast(I32), wb_words[LAST].bitcast(I32))
+
+        def deal_last(rows_no, count, place):
+            tag = "last_codes%d" % rows_no if place == "keep" else place
+            dealt = keep.tile([P, count, 2 * P], U8, name="last_codes", tag=tag, align_bytes=64)
+            g, t = divmod(rows_no, PACK)
+            words = last_raw[0][:].bitcast(U16).rearrange("p (g m t) -> p g t m", g=N_GROUPS, t=PACK)
+            nc.vector.tensor_copy(
+                dealt[:].rearrange("p t w -> p (t w)").bitcast(U16).rearrange("p (t m) -> p t m", t=count),
+                words[:, g, t : t + count, :],
+            )
+            for k in range(count):
+                last_codes[rows_no + k] = dealt[:, k, :]
 
         def quantise_d(rp, after):
             d_codes[rp] = keep.tile([P, S], U32, name="d_codes", tag="prob%d%d" % after, align_bytes=64)
             d_plane[rp] = keep.tile([P, S], U8, name="d_plane%d" % rp, align_bytes=64)
-            for cols in (HALVES[0],) + QUARTERS[2:] if rp == LAST else WHOLE:
+            for piece, cols in enumerate((HALVES[0],) + QUARTERS[2:] if rp == LAST else WHOLE):
+                if rp == LAST and piece != 1:
+                    deal_last(piece, 2, "keep")
                 nc.vector.quantize_mx(
                     d_codes[rp][:, cols].bitcast(FP8X4),
                     d_plane[rp][:, cols],
                     d_round[rp][:, cols, :].rearrange("p j t -> p (j t)"),
                 )
+            if rp == LAST:
+                deal_last(PACK, PACK, "d_round%d" % LAST)
 
         def back_project(rp, first):
             def one_pass(out, rows_no, cols, start, stop):
                 nc.tensor.matmul_mx(
                     out,
-                    lhsT=wb_codes[:, rp, 2 * P * rows_no : 2 * P * (rows_no + 1)].bitcast(FP4X4),
+                    lhsT=(last_codes[rows_no] if rp == LAST else wb_codes[:, rp, 2 * P * rows_no : 2 * P * (rows_no + 1)]).bitcast(FP4X4),
                     lhsT_scale=wb_planes[:, rp, P * rows_no : P * (rows_no + 1)],
                     rhs=d_codes[rp][:, cols].bitcast(FP8X4),
                     rhs_scale=d_plane[rp][:, cols],
@@ -226,6 +246,8 @@ def tile_list_click_feature_grad_kernel(
             logit_gradient(rp, t)
             if step + LABEL_BUFS < len(order):
                 load_labels(*order[step + LABEL_BUFS])
+            if step + LABEL_BUFS == len(order):
+                load_last_words()
             if rp == LAST and t >= 1:
                 quantise_d(t - 1, (rp, t))
                 back_project(t - 1, t == 1)
@@ -254,15 +276,15 @@ def tile_list_click_feature_grad_kernel(
 
         def round_y(g):
             y_round.append(ring.tile([P, S, PACK], BF16, name="y_round", tag="round", bufs=ROUND_BUFS, align_bytes=64))
-            split = S if g == 0 else HALF
+            split = S if g == 0 else 3 * S // 8
             nc.vector.tensor_copy(
                 y_round[g][:, :split, :].rearrange("p (run near) t -> p run t near", near=NEAR),
                 y[g][:, :, :split].rearrange("p t (run near) -> p run t near", near=NEAR),
             )
-            if split < S:
+            for cols in () if g == 0 else (slice(split, HALF), HALVES[1]):
                 nc.scalar.copy(
-                    y_round[g][:, split:, :].rearrange("p (run near) t -> p run t near", near=NEAR),
-                    y[g][:, :, split:].rearrange("p t (run near) -> p run t near", near=NEAR),
+                    y_round[g][:, cols, :].rearrange("p (run near) t -> p run t near", near=NEAR),
+                    y[g][:, :, cols].rearrange("p t (run near) -> p run t near", near=NEAR),
                 )
 
         def quantise_y(g):

@@ -34,7 +34,7 @@ NEAR = 4
 PSUM_BANKS = 8
 LABEL_BUFS = 8
 ROUND_BUFS = R_PASSES
-MISS_BUFS = 3
+MISS_BUFS = 6
 BIAS_ROWS, WEIGHT_ROWS = slice(12, 24, 4), slice(76, 88, 4)
 
 
@@ -82,11 +82,8 @@ def tile_list_click_feature_grad_kernel(
             nc.sync.dma_start(tab[kp][:], tab_words[kp].rearrange("p x i -> p (x i)").bitcast(I32))
         nc.sync.dma_start(a_raw[1][:], a_rows[1])
 
-        order = [(rp, t) for rp in range(LAST) for t in range(PACK - 1)]
-        for t in range(PACK):
-            order.append((LAST, t))
-            if t < LAST:
-                order.append((t, PACK - 1))
+        order = [(0, 0), (0, 1), (0, 2), (LAST, 0), (1, 2), (1, 0), (1, 1)]
+        order.extend([(0, 3), (LAST, 1), (1, 3), (LAST, 2), (LAST, 3)])
         label_rows = {}
 
         def load_labels(rp, t):
@@ -174,12 +171,12 @@ def tile_list_click_feature_grad_kernel(
         def logit_gradient(rp, t):
             scale = minus_weight[:, t, rp : rp + 1]
             miss = ring.tile([P, S], F32, name="miss", bufs=MISS_BUFS)
-            pieces = {(LAST, PACK - 1): QUARTERS, (LAST, PACK - 2): HALVES}.get((rp, t), WHOLE)
+            pieces = {(LAST, PACK - 1): QUARTERS, (LAST, PACK - 2): HALVES, (LAST - 1, PACK - 1): HALVES}.get((rp, t), WHOLE)
             for cols in pieces:
                 picked = label_rows[rp, t][:].indirect(offsets[:, cols.start // 16 : cols.stop // 16])
                 nc.vector.tensor_tensor(miss[:, cols], picked, prob[rp, t][:, cols], ALU.subtract)
             for cols in pieces:
-                if rp == 0 and t < 2:
+                if rp == 1 and t < 2:
                     nc.vector.tensor_scalar(d_round[rp][:, cols, t], miss[:, cols], scale, None, ALU.mult)
                 else:
                     nc.scalar.activation(d_round[rp][:, cols, t], miss[:, cols], ACT.Copy, scale=scale)

@@ -32,7 +32,6 @@ QUARTERS = tuple(slice(q * S // 4, (q + 1) * S // 4) for q in range(4))
 WHOLE = (slice(0, S),)
 NEAR = 4
 PSUM_BANKS = 8
-LABEL_BUFS = 8
 ROUND_BUFS = R_PASSES
 MISS_BUFS = 6
 BIAS_ROWS, WEIGHT_ROWS = slice(12, 24, 4), slice(76, 88, 4)
@@ -74,25 +73,26 @@ def tile_list_click_feature_grad_kernel(
 
         wb_raw = keep.tile([P, LAST, 2 * N], U8, name="wb_raw", align_bytes=64)
         nc.sync.dma_start(wb_raw[:].bitcast(I32), wb_words[:LAST].rearrange("rp p w -> p rp w").bitcast(I32))
-        a_raw = [ring.tile([P, PACK, H], F32, name="a_raw", tag="wide") for kp in range(K_PASSES)]
+        a_raw = [keep.tile([P, PACK, H], F32, name="a_raw", tag="wide%d" % kp, align_bytes=64) for kp in range(K_PASSES)]
         tab = [keep.tile([P, T], I32, name="tab%d" % kp, align_bytes=64) for kp in range(K_PASSES)]
         a_rows = a.rearrange("(kp p i) r -> kp p i r", p=P, i=PACK)
-        nc.sync.dma_start(a_raw[0][:], a_rows[0])
+        for kp in range(K_PASSES):
+            nc.sync.dma_start(a_raw[kp][:], a_rows[kp])
         for kp in range(K_PASSES):
             nc.sync.dma_start(tab[kp][:], tab_words[kp].rearrange("p x i -> p (x i)").bitcast(I32))
-        nc.sync.dma_start(a_raw[1][:], a_rows[1])
 
-        order = [(0, 0), (0, 1), (0, 2), (LAST, 0), (1, 2), (1, 0), (1, 1)]
-        order.extend([(0, 3), (LAST, 1), (1, 3), (LAST, 2), (LAST, 3)])
+        loads = [(0, 0, 2), (0, 2, 2), (1, 0, 2), (1, 2, 1), (1, 3, 1)] + [(LAST, t, 1) for t in range(PACK)]
+        places = ["label0", "label1", "label2", "wide0", "wide1", "label0", "label1", "label2", "wide0"]
         label_rows = {}
 
-        def load_labels(rp, t):
-            label_rows[rp, t] = ring.tile([P, T], F32, name="label_rows", bufs=LABEL_BUFS, align_bytes=64)
-            rows = gT[rp * PASS : (rp + 1) * PASS, :].rearrange("(p t) x -> p t x", t=PACK)
-            nc.sync.dma_start(label_rows[rp, t][:], rows[:, t, :])
+        def load_labels(step):
+            rp, t, count = loads[step]
+            label_rows[rp, t] = keep.tile([P, count * T], F32, name="label_rows", tag=places[step], align_bytes=64)
+            rows = gT[rp * PASS : (rp + 1) * PASS, :].rearrange("(p t) x -> p (t x)", t=PACK)
+            nc.sync.dma_start(label_rows[rp, t][:], rows[:, t * T : (t + count) * T])
 
-        for rp, t in order[:LABEL_BUFS]:
-            load_labels(rp, t)
+        for step in range(3):
+            load_labels(step)
 
         wb_codes = keep.tile([P, LAST, 2 * N], U8, name="wb_codes", align_bytes=64)
         nc.vector.tensor_copy(
@@ -134,6 +134,7 @@ def tile_list_click_feature_grad_kernel(
                 quantise_a(kp, rp)
 
         prepare_a(0)
+        prepare_a(1)
 
         v_codes = [keep.tile([P, S], U32, name="v_codes%d" % kp, align_bytes=64) for kp in range(K_PASSES)]
         for kp in range(K_PASSES):
@@ -146,7 +147,8 @@ def tile_list_click_feature_grad_kernel(
             wb_scale_rows[:].rearrange("p rp (g m t) -> p (rp g) t m", g=N_GROUPS, t=PACK),
         )
 
-        prepare_a(1)
+        load_labels(3)
+        load_labels(4)
 
         for rp in range(R_PASSES):
             for t in range(PACK):
@@ -165,26 +167,42 @@ def tile_list_click_feature_grad_kernel(
                 prob[rp, t] = keep.tile([P, S], F32, name="prob%d%d" % (rp, t), align_bytes=64)
                 nc.scalar.activation(prob[rp, t][:], logits[:], ACT.Sigmoid, bias=bias[:, t, rp : rp + 1])
 
-        d_round = [keep.tile([P, S, PACK], BF16, name="d_round%d" % rp, align_bytes=64) for rp in range(R_PASSES)]
+        d_round = {LAST: keep.tile([P, S, PACK], BF16, name="d_round%d" % LAST, align_bytes=64)}
+        d_pairs = [keep.tile([P, 2, S, 2], BF16, name="d_pairs%d" % rp, align_bytes=64) for rp in range(LAST)]
         y_banks = [psum.tile([P, S], F32, name="bank") for bank_no in range(N_GROUPS * PACK)]
 
-        def logit_gradient(rp, t):
+        def pair_gradient(rp, t):
+            miss = [ring.tile([P, S], F32, name="miss", bufs=MISS_BUFS) for row in range(2)]
+            picked = keep.tile([P, S], F32, name="picked", tag="tab_scale_rows", align_bytes=64)
+            nc.vector.tensor_copy(picked[:], label_rows[rp, t][:, T:].indirect(offsets[:]))
+            nc.vector.tensor_tensor(miss[0][:], label_rows[rp, t][:].indirect(offsets[:]), prob[rp, t][:], ALU.subtract)
+            nc.vector.tensor_tensor(miss[1][:], picked[:], prob[rp, t + 1][:], ALU.subtract)
+            for row in range(2):
+                scale = minus_weight[:, t + row, rp : rp + 1]
+                nc.scalar.activation(d_pairs[rp][:, t // 2, :, row], miss[row][:], ACT.Copy, scale=scale)
+
+        def weave(rp):
+            d_round[rp] = keep.tile([P, S, PACK], BF16, name="d_round%d" % rp, align_bytes=64)
+            nc.scalar.copy(
+                d_round[rp][:].rearrange("p j t -> p (j t)").bitcast(U32).rearrange("p (j u) -> p j u", u=2),
+                d_pairs[rp][:].rearrange("p u j e -> p (u j e)").bitcast(U32).rearrange("p (u j) -> p j u", u=2),
+            )
+
+        def row_gradient(rp, t):
             scale = minus_weight[:, t, rp : rp + 1]
             miss = ring.tile([P, S], F32, name="miss", bufs=MISS_BUFS)
-            pieces = {(LAST, PACK - 1): QUARTERS, (LAST, PACK - 2): HALVES, (LAST - 1, PACK - 1): HALVES}.get((rp, t), WHOLE)
+            pieces = {(LAST, PACK - 1): QUARTERS, (LAST, PACK - 2): HALVES}.get((rp, t), WHOLE)
             for cols in pieces:
                 picked = label_rows[rp, t][:].indirect(offsets[:, cols.start // 16 : cols.stop // 16])
                 nc.vector.tensor_tensor(miss[:, cols], picked, prob[rp, t][:, cols], ALU.subtract)
             for cols in pieces:
-                if rp == 1 and t < 2:
-                    nc.vector.tensor_scalar(d_round[rp][:, cols, t], miss[:, cols], scale, None, ALU.mult)
-                else:
-                    nc.scalar.activation(d_round[rp][:, cols, t], miss[:, cols], ACT.Copy, scale=scale)
+                place = d_round[rp][:, cols, t] if rp == LAST else d_pairs[rp][:, t // 2, cols, t % 2]
+                nc.scalar.activation(place, miss[:, cols], ACT.Copy, scale=scale)
 
         d_codes, d_plane, last_codes, last_raw = {}, {}, {}, []
 
         def load_last_words():
-            last_raw.append(ring.tile([P, 2 * N], U8, name="last_raw", tag="label_rows", bufs=LABEL_BUFS, align_bytes=64))
+            last_raw.append(keep.tile([P, 2 * N], U8, name="last_raw", tag="prob13", align_bytes=64))
             nc.sync.dma_start(last_raw[0][:].bitcast(I32), wb_words[LAST].bitcast(I32))
 
         def deal_last(rows_no, count, place):
@@ -239,12 +257,17 @@ def tile_list_click_feature_grad_kernel(
             for bank_no in range(2, N_GROUPS * PACK):
                 one_pass(y_banks[bank_no][:], bank_no, WHOLE[0], first, rp == LAST)
 
-        for step, (rp, t) in enumerate(order):
-            logit_gradient(rp, t)
-            if step + LABEL_BUFS < len(order):
-                load_labels(*order[step + LABEL_BUFS])
-            if step + LABEL_BUFS == len(order):
+        for step, (rp, t, count) in enumerate(loads):
+            if count == 2:
+                pair_gradient(rp, t)
+            else:
+                row_gradient(rp, t)
+            if step < 4:
+                load_labels(5 + step)
+            if step == 4:
                 load_last_words()
+            if rp < LAST and t + count == PACK:
+                weave(rp)
             if rp == LAST and t >= 1:
                 quantise_d(t - 1, (rp, t))
                 back_project(t - 1, t == 1)
@@ -253,7 +276,7 @@ def tile_list_click_feature_grad_kernel(
         y, y_round = [], []
 
         def empty_banks(g):
-            y.append(ring.tile([P, PACK, S], F32, name="y", tag="wide"))
+            y.append(keep.tile([P, PACK, S], F32, name="y", tag="wide%d" % g, align_bytes=64))
             rows = out_0[g * PASS : (g + 1) * PASS, :].rearrange("(p t) j -> p t j", t=PACK)
             for t in range(PACK):
                 bank = y_banks[g * PACK + t]

@@ -30,6 +30,7 @@ HALF = S // 2
 HALVES = (slice(0, HALF), slice(HALF, S))
 QUARTERS = tuple(slice(q * S // 4, (q + 1) * S // 4) for q in range(4))
 WHOLE = (slice(0, S),)
+ROW_PAIRS = (slice(0, 2), slice(2, 4))
 NEAR = 4
 PSUM_BANKS = 8
 ROUND_BUFS = R_PASSES
@@ -76,10 +77,11 @@ def tile_list_click_feature_grad_kernel(
         a_raw = [keep.tile([P, PACK, H], F32, name="a_raw", tag="wide%d" % kp, align_bytes=64) for kp in range(K_PASSES)]
         tab = [keep.tile([P, T], I32, name="tab%d" % kp, align_bytes=64) for kp in range(K_PASSES)]
         a_rows = a.rearrange("(kp p i) r -> kp p i r", p=P, i=PACK)
-        for kp in range(K_PASSES):
-            nc.sync.dma_start(a_raw[kp][:], a_rows[kp])
+        nc.sync.dma_start(a_raw[0][:], a_rows[0])
         for kp in range(K_PASSES):
             nc.sync.dma_start(tab[kp][:], tab_words[kp].rearrange("p x i -> p (x i)").bitcast(I32))
+        for pair in ROW_PAIRS:
+            nc.sync.dma_start(a_raw[1][:, pair, :], a_rows[1][:, pair, :])
 
         loads = [(0, 0, 2), (0, 2, 2), (1, 0, 2), (1, 2, 1), (1, 3, 1)] + [(LAST, t, 1) for t in range(PACK)]
         places = ["label0", "label1", "label2", "wide0", "wide1", "label0", "label1", "label2", "wide0"]
@@ -112,29 +114,23 @@ def tile_list_click_feature_grad_kernel(
 
         a_round, a_codes, a_planes, prob = {}, {}, {}, {}
 
-        def round_a(kp, rp):
-            a_round[kp, rp] = ring.tile([P, PACK * PASS], BF16, name="a_round", tag="round", bufs=ROUND_BUFS, align_bytes=64)
+        def round_a(kp, rp, rows, engine_copy):
+            if (kp, rp) not in a_round:
+                a_round[kp, rp] = ring.tile([P, PACK * PASS], BF16, name="a_round", tag="round", bufs=ROUND_BUFS, align_bytes=64)
             dealt = a_round[kp, rp][:].rearrange("p (u e m i) -> p u m i e", u=2, e=2, i=PACK)
             block = a_raw[kp][:, :, rp * PASS : (rp + 1) * PASS].rearrange("p i (m u e) -> p u m i e", u=2, e=2)
             for u in range(2):
-                if rp == LAST:
-                    nc.scalar.copy(dealt[:, u], block[:, u])
-                else:
-                    nc.vector.tensor_copy(dealt[:, u], block[:, u])
+                engine_copy(dealt[:, u, :, rows, :], block[:, u, :, rows, :])
 
         def quantise_a(kp, rp):
             a_codes[kp, rp] = keep.tile([P, PASS], U32, name="a_codes%d%d" % (kp, rp), align_bytes=64)
             a_planes[kp, rp] = keep.tile([P, PASS], U8, name="a_planes%d%d" % (kp, rp), align_bytes=64)
             nc.vector.quantize_mx(a_codes[kp, rp][:].bitcast(FP8X4), a_planes[kp, rp][:], a_round[kp, rp][:])
 
-        def prepare_a(kp):
-            for rp in range(R_PASSES):
-                round_a(kp, rp)
-            for rp in range(R_PASSES):
-                quantise_a(kp, rp)
-
-        prepare_a(0)
-        prepare_a(1)
+        for rp in range(R_PASSES):
+            round_a(0, rp, slice(0, PACK), nc.scalar.copy if rp == LAST else nc.vector.tensor_copy)
+        for rp in range(R_PASSES):
+            quantise_a(0, rp)
 
         v_codes = [keep.tile([P, S], U32, name="v_codes%d" % kp, align_bytes=64) for kp in range(K_PASSES)]
         for kp in range(K_PASSES):
@@ -148,6 +144,12 @@ def tile_list_click_feature_grad_kernel(
         )
 
         load_labels(3)
+        for rp in range(R_PASSES):
+            round_a(1, rp, ROW_PAIRS[0], nc.vector.tensor_copy if rp == LAST else nc.scalar.copy)
+        for rp in range(R_PASSES):
+            round_a(1, rp, ROW_PAIRS[1], nc.scalar.copy if rp == LAST else nc.vector.tensor_copy)
+        for rp in range(R_PASSES):
+            quantise_a(1, rp)
         load_labels(4)
 
         for rp in range(R_PASSES):
@@ -191,7 +193,7 @@ def tile_list_click_feature_grad_kernel(
         def row_gradient(rp, t):
             scale = minus_weight[:, t, rp : rp + 1]
             miss = ring.tile([P, S], F32, name="miss", bufs=MISS_BUFS)
-            pieces = {(LAST, PACK - 1): QUARTERS, (LAST, PACK - 2): HALVES}.get((rp, t), WHOLE)
+            pieces = {(LAST, PACK - 1): QUARTERS, (LAST, PACK - 2): HALVES, (LAST, PACK - 3): HALVES}.get((rp, t), WHOLE)
             for cols in pieces:
                 picked = label_rows[rp, t][:].indirect(offsets[:, cols.start // 16 : cols.stop // 16])
                 nc.vector.tensor_tensor(miss[:, cols], picked, prob[rp, t][:, cols], ALU.subtract)
@@ -257,6 +259,7 @@ def tile_list_click_feature_grad_kernel(
             for bank_no in range(2, N_GROUPS * PACK):
                 one_pass(y_banks[bank_no][:], bank_no, WHOLE[0], first, rp == LAST)
 
+        closing = {0: 0, 2: 1, 3: LAST}
         for step, (rp, t, count) in enumerate(loads):
             if count == 2:
                 pair_gradient(rp, t)
@@ -268,9 +271,9 @@ def tile_list_click_feature_grad_kernel(
                 load_last_words()
             if rp < LAST and t + count == PACK:
                 weave(rp)
-            if rp == LAST and t >= 1:
-                quantise_d(t - 1, (rp, t))
-                back_project(t - 1, t == 1)
+            if rp == LAST and t in closing:
+                quantise_d(closing[t], (rp, t))
+                back_project(closing[t], closing[t] == 0)
 
         y_planes = keep.tile([P, N_GROUPS, S], U8, name="y_planes", align_bytes=64)
         y, y_round = [], []

@@ -83,8 +83,8 @@ def tile_list_click_feature_grad_kernel(
         for pair in ROW_PAIRS:
             nc.sync.dma_start(a_raw[1][:, pair, :], a_rows[1][:, pair, :])
 
-        loads = [(0, 0, 2), (0, 2, 2), (1, 0, 2), (1, 2, 1), (1, 3, 1)] + [(LAST, t, 1) for t in range(PACK)]
-        places = ["label0", "label1", "label2", "wide0", "wide1", "label0", "label1", "label2", "wide0"]
+        loads = [(rp, t, 1) for rp in range(R_PASSES) for t in range(PACK)]
+        places = ["label%d" % k for k in range(6)] + ["wide0", "wide1"] + ["label%d" % k for k in range(4)]
         label_rows = {}
 
         def load_labels(step):
@@ -93,14 +93,24 @@ def tile_list_click_feature_grad_kernel(
             rows = gT[rp * PASS : (rp + 1) * PASS, :].rearrange("(p t) x -> p (t x)", t=PACK)
             nc.sync.dma_start(label_rows[rp, t][:], rows[:, t * T : (t + count) * T])
 
-        for step in range(3):
+        for step in range(6):
             load_labels(step)
 
-        wb_codes = keep.tile([P, LAST, 2 * N], U8, name="wb_codes", align_bytes=64)
-        nc.vector.tensor_copy(
-            wb_codes[:].bitcast(U16).rearrange("p rp (g t m) -> p (rp g) t m", g=N_GROUPS, t=PACK),
-            wb_raw[:].bitcast(U16).rearrange("p rp (g m t) -> p (rp g) t m", g=N_GROUPS, t=PACK),
-        )
+        wb_codes = {}
+
+        def deal_words(rp, raw, rows_no, count, tag):
+            dealt = keep.tile([P, count, 2 * P], U8, name="wb_dealt", tag=tag, align_bytes=64)
+            g, t = divmod(rows_no, PACK)
+            words = raw.bitcast(U16).rearrange("p (g m t) -> p g t m", g=N_GROUPS, t=PACK)
+            nc.vector.tensor_copy(
+                dealt[:].rearrange("p t w -> p (t w)").bitcast(U16).rearrange("p (t m) -> p t m", t=count),
+                words[:, g, t : t + count, :],
+            )
+            for k in range(count):
+                wb_codes[rp, rows_no + k] = dealt[:, k, :]
+
+        for rp, g in ((0, 0), (0, 1), (1, 0)):
+            deal_words(rp, wb_raw[:, rp, :], g * PACK, PACK, "wb_codes%d%d" % (rp, g))
 
         turned = psum.tile([P, PACK, P], F32, name="bank")
         for t in range(PACK):
@@ -143,14 +153,14 @@ def tile_list_click_feature_grad_kernel(
             wb_scale_rows[:].rearrange("p rp (g m t) -> p (rp g) t m", g=N_GROUPS, t=PACK),
         )
 
-        load_labels(3)
+        load_labels(6)
         for rp in range(R_PASSES):
             round_a(1, rp, ROW_PAIRS[0], nc.vector.tensor_copy if rp == LAST else nc.scalar.copy)
         for rp in range(R_PASSES):
             round_a(1, rp, ROW_PAIRS[1], nc.scalar.copy if rp == LAST else nc.vector.tensor_copy)
         for rp in range(R_PASSES):
             quantise_a(1, rp)
-        load_labels(4)
+        load_labels(7)
 
         for rp in range(R_PASSES):
             for t in range(PACK):
@@ -173,16 +183,6 @@ def tile_list_click_feature_grad_kernel(
         d_pairs = [keep.tile([P, 2, S, 2], BF16, name="d_pairs%d" % rp, align_bytes=64) for rp in range(LAST)]
         y_banks = [psum.tile([P, S], F32, name="bank") for bank_no in range(N_GROUPS * PACK)]
 
-        def pair_gradient(rp, t):
-            miss = [ring.tile([P, S], F32, name="miss", bufs=MISS_BUFS) for row in range(2)]
-            picked = keep.tile([P, S], F32, name="picked", tag="tab_scale_rows", align_bytes=64)
-            nc.vector.tensor_copy(picked[:], label_rows[rp, t][:, T:].indirect(offsets[:]))
-            nc.vector.tensor_tensor(miss[0][:], label_rows[rp, t][:].indirect(offsets[:]), prob[rp, t][:], ALU.subtract)
-            nc.vector.tensor_tensor(miss[1][:], picked[:], prob[rp, t + 1][:], ALU.subtract)
-            for row in range(2):
-                scale = minus_weight[:, t + row, rp : rp + 1]
-                nc.scalar.activation(d_pairs[rp][:, t // 2, :, row], miss[row][:], ACT.Copy, scale=scale)
-
         def weave(rp):
             d_round[rp] = keep.tile([P, S, PACK], BF16, name="d_round%d" % rp, align_bytes=64)
             nc.scalar.copy(
@@ -201,43 +201,33 @@ def tile_list_click_feature_grad_kernel(
                 place = d_round[rp][:, cols, t] if rp == LAST else d_pairs[rp][:, t // 2, cols, t % 2]
                 nc.scalar.activation(place, miss[:, cols], ACT.Copy, scale=scale)
 
-        d_codes, d_plane, last_codes, last_raw = {}, {}, {}, []
+        d_codes, d_plane, last_raw = {}, {}, []
 
         def load_last_words():
-            last_raw.append(keep.tile([P, 2 * N], U8, name="last_raw", tag="prob13", align_bytes=64))
+            last_raw.append(keep.tile([P, 2 * N], U8, name="last_raw", tag="prob10", align_bytes=64))
             nc.sync.dma_start(last_raw[0][:].bitcast(I32), wb_words[LAST].bitcast(I32))
-
-        def deal_last(rows_no, count, place):
-            tag = "last_codes%d" % rows_no if place == "keep" else place
-            dealt = keep.tile([P, count, 2 * P], U8, name="last_codes", tag=tag, align_bytes=64)
-            g, t = divmod(rows_no, PACK)
-            words = last_raw[0][:].bitcast(U16).rearrange("p (g m t) -> p g t m", g=N_GROUPS, t=PACK)
-            nc.vector.tensor_copy(
-                dealt[:].rearrange("p t w -> p (t w)").bitcast(U16).rearrange("p (t m) -> p t m", t=count),
-                words[:, g, t : t + count, :],
-            )
-            for k in range(count):
-                last_codes[rows_no + k] = dealt[:, k, :]
 
         def quantise_d(rp, after):
             d_codes[rp] = keep.tile([P, S], U32, name="d_codes", tag="prob%d%d" % after, align_bytes=64)
             d_plane[rp] = keep.tile([P, S], U8, name="d_plane%d" % rp, align_bytes=64)
             for piece, cols in enumerate((HALVES[0],) + QUARTERS[2:] if rp == LAST else WHOLE):
                 if rp == LAST and piece != 1:
-                    deal_last(piece, 2, "keep")
+                    deal_words(LAST, last_raw[0][:], piece, 2, "last_codes%d" % piece)
                 nc.vector.quantize_mx(
                     d_codes[rp][:, cols].bitcast(FP8X4),
                     d_plane[rp][:, cols],
                     d_round[rp][:, cols, :].rearrange("p j t -> p (j t)"),
                 )
             if rp == LAST:
-                deal_last(PACK, PACK, "d_round%d" % LAST)
+                deal_words(LAST, last_raw[0][:], PACK, PACK, "d_round%d" % LAST)
 
-        def back_project(rp, first):
+        def back_project(rp, banks):
+            first = rp == 0
+
             def one_pass(out, rows_no, cols, start, stop):
                 nc.tensor.matmul_mx(
                     out,
-                    lhsT=(last_codes[rows_no] if rp == LAST else wb_codes[:, rp, 2 * P * rows_no : 2 * P * (rows_no + 1)]).bitcast(FP4X4),
+                    lhsT=wb_codes[rp, rows_no].bitcast(FP4X4),
                     lhsT_scale=wb_planes[:, rp, P * rows_no : P * (rows_no + 1)],
                     rhs=d_codes[rp][:, cols].bitcast(FP8X4),
                     rhs_scale=d_plane[rp][:, cols],
@@ -245,7 +235,7 @@ def tile_list_click_feature_grad_kernel(
                     stop=stop,
                 )
 
-            for half in range(2):
+            for half in range(2 if 0 in banks else 0):
                 for q in range(2):
                     for t in range(2):
                         place = t * HALF + q * P
@@ -256,24 +246,24 @@ def tile_list_click_feature_grad_kernel(
                             first and q == 0 and t == 0,
                             rp == LAST and q == 1 and t == 1,
                         )
-            for bank_no in range(2, N_GROUPS * PACK):
+            for bank_no in range(max(2, banks.start), banks.stop):
                 one_pass(y_banks[bank_no][:], bank_no, WHOLE[0], first, rp == LAST)
 
-        closing = {0: 0, 2: 1, 3: LAST}
+        closing = {0: 0, 1: 1, 3: LAST}
         for step, (rp, t, count) in enumerate(loads):
-            if count == 2:
-                pair_gradient(rp, t)
-            else:
-                row_gradient(rp, t)
+            row_gradient(rp, t)
             if step < 4:
-                load_labels(5 + step)
+                load_labels(8 + step)
             if step == 4:
                 load_last_words()
             if rp < LAST and t + count == PACK:
                 weave(rp)
             if rp == LAST and t in closing:
                 quantise_d(closing[t], (rp, t))
-                back_project(closing[t], closing[t] == 0)
+                back_project(closing[t], range(PACK if t == 1 else PSUM_BANKS))
+            if (rp, t) == (LAST, 2):
+                deal_words(1, wb_raw[:, 1, :], PACK, PACK, "prob%d%d" % (rp, t))
+                back_project(1, range(PACK, PSUM_BANKS))
 
         y_planes = keep.tile([P, N_GROUPS, S], U8, name="y_planes", align_bytes=64)
         y, y_round = [], []

@@ -80,8 +80,7 @@ def tile_list_click_feature_grad_kernel(
         nc.sync.dma_start(a_raw[0][:], a_rows[0])
         for kp in range(K_PASSES):
             nc.sync.dma_start(tab[kp][:], tab_words[kp].rearrange("p x i -> p (x i)").bitcast(I32))
-        for pair in ROW_PAIRS:
-            nc.sync.dma_start(a_raw[1][:, pair, :], a_rows[1][:, pair, :])
+        nc.sync.dma_start(a_raw[1][:], a_rows[1])
 
         loads = [(rp, t, 1) for rp in range(R_PASSES) for t in range(PACK)]
         places = ["label%d" % k for k in range(6)] + ["wide0", "wide1"] + ["label%d" % k for k in range(4)]
@@ -117,8 +116,6 @@ def tile_list_click_feature_grad_kernel(
             nc.tensor.transpose(turned[:, t, :], slot_rows[:, t::PACK], identity[:])
         bias = keep.tile([P, PACK, R_PASSES], F32, name="bias")
         minus_weight = keep.tile([P, PACK, R_PASSES], F32, name="minus_weight")
-        warm = keep.tile([P, 1], F32, name="warm")
-        nc.scalar.activation(warm[:], turned[:, 0, 0:1], ACT.Sigmoid)
         nc.scalar.copy(bias[:], turned[:, :, BIAS_ROWS])
         nc.scalar.activation(minus_weight[:], turned[:, :, WEIGHT_ROWS], ACT.Copy, scale=-1.0)
 
@@ -155,9 +152,7 @@ def tile_list_click_feature_grad_kernel(
 
         load_labels(6)
         for rp in range(R_PASSES):
-            round_a(1, rp, ROW_PAIRS[0], nc.vector.tensor_copy if rp == LAST else nc.scalar.copy)
-        for rp in range(R_PASSES):
-            round_a(1, rp, ROW_PAIRS[1], nc.scalar.copy if rp == LAST else nc.vector.tensor_copy)
+            round_a(1, rp, slice(0, PACK), nc.scalar.copy if rp == LAST else nc.vector.tensor_copy)
         for rp in range(R_PASSES):
             quantise_a(1, rp)
         load_labels(7)
@@ -193,7 +188,7 @@ def tile_list_click_feature_grad_kernel(
         def row_gradient(rp, t):
             scale = minus_weight[:, t, rp : rp + 1]
             miss = ring.tile([P, S], F32, name="miss", bufs=MISS_BUFS)
-            pieces = {(LAST, PACK - 1): QUARTERS, (LAST, PACK - 2): HALVES, (LAST, PACK - 3): HALVES}.get((rp, t), WHOLE)
+            pieces = {(LAST, PACK - 1): (slice(0, 64), slice(64, 128)) + QUARTERS[1:], (LAST, PACK - 2): HALVES, (LAST, PACK - 3): HALVES}.get((rp, t), WHOLE)
             for cols in pieces:
                 picked = label_rows[rp, t][:].indirect(offsets[:, cols.start // 16 : cols.stop // 16])
                 nc.vector.tensor_tensor(miss[:, cols], picked, prob[rp, t][:, cols], ALU.subtract)
@@ -210,8 +205,8 @@ def tile_list_click_feature_grad_kernel(
         def quantise_d(rp, after):
             d_codes[rp] = keep.tile([P, S], U32, name="d_codes", tag="prob%d%d" % after, align_bytes=64)
             d_plane[rp] = keep.tile([P, S], U8, name="d_plane%d" % rp, align_bytes=64)
-            for piece, cols in enumerate((HALVES[0],) + QUARTERS[2:] if rp == LAST else WHOLE):
-                if rp == LAST and piece != 1:
+            for piece, cols in enumerate(QUARTERS if rp == LAST else WHOLE):
+                if rp == LAST and piece % 2 == 0:
                     deal_words(LAST, last_raw[0][:], piece, 2, "last_codes%d" % piece)
                 nc.vector.quantize_mx(
                     d_codes[rp][:, cols].bitcast(FP8X4),
@@ -236,17 +231,18 @@ def tile_list_click_feature_grad_kernel(
                 )
 
             for half in range(2 if 0 in banks else 0):
-                for q in range(2):
-                    for t in range(2):
-                        place = t * HALF + q * P
-                        one_pass(
-                            y_banks[half][:, place : place + P],
-                            t,
-                            QUARTERS[2 * half + q],
-                            first and q == 0 and t == 0,
-                            rp == LAST and q == 1 and t == 1,
-                        )
-            for bank_no in range(max(2, banks.start), banks.stop):
+                for pair in range(2):
+                    for q in range(2):
+                        for row in range(2):
+                            place = row * HALF + q * P
+                            one_pass(
+                                y_banks[2 * half + pair][:, place : place + P],
+                                2 * pair + row,
+                                QUARTERS[2 * half + q],
+                                first and q == 0 and row == 0,
+                                rp == LAST and q == 1 and row == 1,
+                            )
+            for bank_no in range(max(PACK, banks.start), banks.stop):
                 one_pass(y_banks[bank_no][:], bank_no, WHOLE[0], first, rp == LAST)
 
         closing = {0: 0, 1: 1, 3: LAST}
@@ -273,14 +269,14 @@ def tile_list_click_feature_grad_kernel(
             rows = out_0[g * PASS : (g + 1) * PASS, :].rearrange("(p t) j -> p t j", t=PACK)
             for t in range(PACK):
                 bank = y_banks[g * PACK + t]
-                if g == 0 and t < 2:
+                if g == 0 and t % 2 == 0:
+                    cols = HALVES[t // 2]
                     for row in range(2):
-                        if t == 0:
-                            nc.scalar.copy(y[g][:, row, HALVES[t]], bank[:, HALVES[row]])
-                        else:
-                            nc.vector.tensor_copy(y[g][:, row, HALVES[t]], bank[:, HALVES[row]])
-                        nc.sync.dma_start(rows[:, row, HALVES[t]], y[g][:, row, HALVES[t]])
-                elif t == 1 or (g == 0 and t == 3):
+                        nc.scalar.copy(y[g][:, row, cols], bank[:, HALVES[row]])
+                        nc.sync.dma_start(rows[:, row, cols], y[g][:, row, cols])
+                elif g == 0:
+                    nc.vector.tensor_copy(y[g][:, 2:, HALVES[t // 2]], bank[:].rearrange("p (row j) -> p row j", row=2))
+                elif t == 1:
                     nc.vector.tensor_copy(y[g][:, t, :], bank[:])
                 else:
                     nc.scalar.copy(y[g][:, t, :], bank[:])

@@ -290,7 +290,7 @@ def tile_list_click_feature_grad_kernel(
                 y_round[g][:, :split, :].rearrange("p (run near) t -> p run t near", near=NEAR),
                 y[g][:, :, :split].rearrange("p t (run near) -> p run t near", near=NEAR),
             )
-            for cols in () if g == 0 else (slice(split, HALF), HALVES[1]):
+            for cols in () if g == 0 else (slice(split, HALF),) + QUARTERS[2:]:
                 nc.scalar.copy(
                     y_round[g][:, cols, :].rearrange("p (run near) t -> p run t near", near=NEAR),
                     y[g][:, :, cols].rearrange("p t (run near) -> p run t near", near=NEAR),
@@ -299,13 +299,13 @@ def tile_list_click_feature_grad_kernel(
         def quantise_y(g):
             y_codes = keep.tile([P, S], U32, name="y_codes%d" % g, align_bytes=64)
             words = out_1[g].rearrange("p j t -> p (j t)").bitcast(I32)
-            for cols in WHOLE if g == 0 else HALVES:
+            for cols in WHOLE if g == 0 else (HALVES[0],) + QUARTERS[2:]:
                 nc.vector.quantize_mx(
                     y_codes[:, cols].bitcast(FP8X4),
                     y_planes[:, g, cols],
                     y_round[g][:, cols, :].rearrange("p j t -> p (j t)"),
                 )
-                nc.sync.dma_start(words[:, cols], y_codes[:, cols].bitcast(I32))
+            nc.sync.dma_start(words, y_codes[:].bitcast(I32))
 
         for stage in (empty_banks, round_y, quantise_y):
             for g in range(N_GROUPS):

@@ -171,8 +171,11 @@ def tile_list_click_feature_grad_kernel(
                         start=(kp == 0),
                         stop=(kp == K_PASSES - 1),
                     )
-                prob[rp, t] = keep.tile([P, S], F32, name="prob%d%d" % (rp, t), align_bytes=64)
-                nc.scalar.activation(prob[rp, t][:], logits[:], ACT.Sigmoid, bias=bias[:, t, rp : rp + 1])
+                for cols in HALVES if (rp, t) == (LAST, 0) else WHOLE:
+                    name = "prob%d%d" % (rp, t) if cols.start == 0 else "prob_rest"
+                    part = keep.tile([P, cols.stop - cols.start], F32, name=name, align_bytes=64)
+                    nc.scalar.activation(part[:], logits[:, cols], ACT.Sigmoid, bias=bias[:, t, rp : rp + 1])
+                    prob[rp, t, cols.start] = part
 
         d_round = {LAST: keep.tile([P, S, PACK], BF16, name="d_round%d" % LAST, align_bytes=64)}
         d_pairs = [keep.tile([P, 2, S, 2], BF16, name="d_pairs%d" % rp, align_bytes=64) for rp in range(LAST)]
@@ -188,10 +191,11 @@ def tile_list_click_feature_grad_kernel(
         def row_gradient(rp, t):
             scale = minus_weight[:, t, rp : rp + 1]
             miss = ring.tile([P, S], F32, name="miss", bufs=MISS_BUFS)
-            pieces = {(LAST, PACK - 1): (slice(0, 64), slice(64, 128)) + QUARTERS[1:], (LAST, PACK - 2): HALVES, (LAST, PACK - 3): HALVES}.get((rp, t), WHOLE)
+            pieces = {(LAST, PACK - 1): (slice(0, 64), slice(64, 128)) + QUARTERS[1:], (LAST, PACK - 2): QUARTERS, (LAST, PACK - 3): HALVES, (LAST, 0): HALVES}.get((rp, t), WHOLE)
             for cols in pieces:
                 picked = label_rows[rp, t][:].indirect(offsets[:, cols.start // 16 : cols.stop // 16])
-                nc.vector.tensor_tensor(miss[:, cols], picked, prob[rp, t][:, cols], ALU.subtract)
+                part = prob[rp, t, cols.start][:] if (rp, t) == (LAST, 0) else prob[rp, t, 0][:, cols]
+                nc.vector.tensor_tensor(miss[:, cols], picked, part, ALU.subtract)
             for cols in pieces:
                 place = d_round[rp][:, cols, t] if rp == LAST else d_pairs[rp][:, t // 2, cols, t % 2]
                 nc.scalar.activation(place, miss[:, cols], ACT.Copy, scale=scale)

@@ -266,7 +266,7 @@ def tile_list_click_feature_grad_kernel(
                 back_project(1, range(PACK, PSUM_BANKS))
 
         y_planes = keep.tile([P, N_GROUPS, S], U8, name="y_planes", align_bytes=64)
-        y, y_round = [], []
+        y, y_round, early = [], [], []
 
         def empty_banks(g):
             y.append(keep.tile([P, PACK, S], F32, name="y", tag="wide%d" % g, align_bytes=64))
@@ -280,21 +280,27 @@ def tile_list_click_feature_grad_kernel(
                         nc.sync.dma_start(rows[:, row, cols], y[g][:, row, cols])
                 elif g == 0:
                     nc.vector.tensor_copy(y[g][:, 2:, HALVES[t // 2]], bank[:].rearrange("p (row j) -> p row j", row=2))
-                elif t == 1:
+                elif t < 2:
                     nc.vector.tensor_copy(y[g][:, t, :], bank[:])
                 else:
                     nc.scalar.copy(y[g][:, t, :], bank[:])
-                if t % 2 == 1 and (g, t) != (0, 1):
+                if (g, t) == (0, 3):
                     nc.sync.dma_start(rows[:, t - 1 : t + 1, :], y[g][:, t - 1 : t + 1, :])
+                if (g, t) == (1, 3):
+                    nc.sync.dma_start(rows, y[g][:])
 
         def round_y(g):
             y_round.append(ring.tile([P, S, PACK], BF16, name="y_round", tag="round", bufs=ROUND_BUFS, align_bytes=64))
-            split = S if g == 0 else 3 * S // 8
+            split = S if g == 0 else S // 4
+            first = HALF if g == 0 else 0
+            if g == 0:
+                early.append(keep.tile([P, HALF, PACK], BF16, name="y_early", tag="prob10", align_bytes=64))
+                nc.gpsimd.tensor_scalar(early[0][:], y[g][:, :, :HALF].rearrange("p t j -> p j t"), 1.0, 0.0, ALU.mult, ALU.add)
             nc.vector.tensor_copy(
-                y_round[g][:, :split, :].rearrange("p (run near) t -> p run t near", near=NEAR),
-                y[g][:, :, :split].rearrange("p t (run near) -> p run t near", near=NEAR),
+                y_round[g][:, first:split, :].rearrange("p (run near) t -> p run t near", near=NEAR),
+                y[g][:, :, first:split].rearrange("p t (run near) -> p run t near", near=NEAR),
             )
-            for cols in () if g == 0 else (slice(split, HALF),) + QUARTERS[2:]:
+            for cols in () if g == 0 else QUARTERS[1:]:
                 nc.scalar.copy(
                     y_round[g][:, cols, :].rearrange("p (run near) t -> p run t near", near=NEAR),
                     y[g][:, :, cols].rearrange("p t (run near) -> p run t near", near=NEAR),
@@ -303,11 +309,11 @@ def tile_list_click_feature_grad_kernel(
         def quantise_y(g):
             y_codes = keep.tile([P, S], U32, name="y_codes%d" % g, align_bytes=64)
             words = out_1[g].rearrange("p j t -> p (j t)").bitcast(I32)
-            for cols in WHOLE if g == 0 else (HALVES[0],) + QUARTERS[2:]:
+            for cols in HALVES if g == 0 else (HALVES[0],) + QUARTERS[2:]:
                 nc.vector.quantize_mx(
                     y_codes[:, cols].bitcast(FP8X4),
                     y_planes[:, g, cols],
-                    y_round[g][:, cols, :].rearrange("p j t -> p (j t)"),
+                    (early[0][:] if (g, cols.start) == (0, 0) else y_round[g][:, cols, :]).rearrange("p j t -> p (j t)"),
                 )
             nc.sync.dma_start(words, y_codes[:].bitcast(I32))
 

@@ -29,12 +29,16 @@ LAST = R_PASSES - 1
 HALF = S // 2
 HALVES = (slice(0, HALF), slice(HALF, S))
 QUARTERS = tuple(slice(q * S // 4, (q + 1) * S // 4) for q in range(4))
+EIGHTHS = (slice(0, S // 8), slice(S // 8, S // 4))
 WHOLE = (slice(0, S),)
-ROW_PAIRS = (slice(0, 2), slice(2, 4))
+LAST_PIECES = (HALVES, HALVES, QUARTERS, EIGHTHS + QUARTERS[1:])
+PARK_STEP = 8
 NEAR = 4
 PSUM_BANKS = 8
 ROUND_BUFS = R_PASSES
 MISS_BUFS = 6
+LABEL_PLACES = 6
+VECTOR_ROUNDS = S // 4
 BIAS_ROWS, WEIGHT_ROWS = slice(12, 24, 4), slice(76, 88, 4)
 
 
@@ -48,10 +52,9 @@ def tile_list_click_feature_grad_kernel(
         psum = ctx.enter_context(tc.psum_pool(name="psum", bufs=PSUM_BANKS))
 
         offsets = keep.tile([P, S // 16], U16, name="offsets")
-        nc.sync.dma_start(offsets[:], offs)
 
         tab_scale_rows = keep.tile([P, T], U8, name="tab_scale_rows", align_bytes=64)
-        wb_scale_rows = keep.tile([P, R_PASSES, N], U8, name="wb_scale_rows", align_bytes=64)
+        wb_scale_rows = keep.tile([P, LAST, N], U8, name="wb_scale_rows", align_bytes=64)
         slot_rows = keep.tile([P, PASS], F32, name="slot_rows")
         identity = keep.tile([P, P], F32, name="identity")
         nc.gpsimd.memset(slot_rows[:], 0.0)
@@ -69,11 +72,13 @@ def tile_list_click_feature_grad_kernel(
         for row in range(QUAD_ROWS):
             nc.scalar.dma_start(
                 wb_scale_rows[row:P:32, :, :].bitcast(I32),
-                wb_scales[:, row::QUAD_ROWS, :].rearrange("rp quad n -> quad rp n").bitcast(I32),
+                wb_scales[:LAST, row::QUAD_ROWS, :].rearrange("rp quad n -> quad rp n").bitcast(I32),
             )
+        nc.gpsimd.dma_start(wb_scale_rows[QUAD_ROWS:P:PARK_STEP, 0, :].bitcast(I32), wb_scales[LAST].bitcast(I32))
 
         wb_raw = keep.tile([P, LAST, 2 * N], U8, name="wb_raw", align_bytes=64)
         nc.sync.dma_start(wb_raw[:].bitcast(I32), wb_words[:LAST].rearrange("rp p w -> p rp w").bitcast(I32))
+        nc.sync.dma_start(offsets[:], offs)
         a_raw = [keep.tile([P, PACK, H], F32, name="a_raw", tag="wide%d" % kp, align_bytes=64) for kp in range(K_PASSES)]
         tab = [keep.tile([P, T], I32, name="tab%d" % kp, align_bytes=64) for kp in range(K_PASSES)]
         a_rows = a.rearrange("(kp p i) r -> kp p i r", p=P, i=PACK)
@@ -82,17 +87,19 @@ def tile_list_click_feature_grad_kernel(
             nc.sync.dma_start(tab[kp][:], tab_words[kp].rearrange("p x i -> p (x i)").bitcast(I32))
         nc.sync.dma_start(a_raw[1][:], a_rows[1])
 
-        loads = [(rp, t, 1) for rp in range(R_PASSES) for t in range(PACK)]
-        places = ["label%d" % k for k in range(6)] + ["wide0", "wide1"] + ["label%d" % k for k in range(4)]
+        loads = [(rp, t) for rp in range(R_PASSES) for t in range(PACK)]
+        own_places = ["label%d" % k for k in range(LABEL_PLACES)]
+        first_places = own_places + ["wide%d" % kp for kp in range(K_PASSES)]
+        places = (first_places + own_places)[: len(loads)]
         label_rows = {}
 
         def load_labels(step):
-            rp, t, count = loads[step]
-            label_rows[rp, t] = keep.tile([P, count * T], F32, name="label_rows", tag=places[step], align_bytes=64)
+            rp, t = loads[step]
+            label_rows[rp, t] = keep.tile([P, T], F32, name="label_rows", tag=places[step], align_bytes=64)
             rows = gT[rp * PASS : (rp + 1) * PASS, :].rearrange("(p t) x -> p (t x)", t=PACK)
-            nc.sync.dma_start(label_rows[rp, t][:], rows[:, t * T : (t + count) * T])
+            nc.sync.dma_start(label_rows[rp, t][:], rows[:, t * T : (t + 1) * T])
 
-        for step in range(6):
+        for step in range(LABEL_PLACES):
             load_labels(step)
 
         wb_codes = {}
@@ -121,13 +128,13 @@ def tile_list_click_feature_grad_kernel(
 
         a_round, a_codes, a_planes, prob = {}, {}, {}, {}
 
-        def round_a(kp, rp, rows, engine_copy):
-            if (kp, rp) not in a_round:
-                a_round[kp, rp] = ring.tile([P, PACK * PASS], BF16, name="a_round", tag="round", bufs=ROUND_BUFS, align_bytes=64)
+        def round_a(kp, rp):
+            engine_copy = nc.scalar.copy if rp == LAST else nc.vector.tensor_copy
+            a_round[kp, rp] = ring.tile([P, PACK * PASS], BF16, name="a_round", tag="round", bufs=ROUND_BUFS, align_bytes=64)
             dealt = a_round[kp, rp][:].rearrange("p (u e m i) -> p u m i e", u=2, e=2, i=PACK)
             block = a_raw[kp][:, :, rp * PASS : (rp + 1) * PASS].rearrange("p i (m u e) -> p u m i e", u=2, e=2)
             for u in range(2):
-                engine_copy(dealt[:, u, :, rows, :], block[:, u, :, rows, :])
+                engine_copy(dealt[:, u, :, :, :], block[:, u, :, :, :])
 
         def quantise_a(kp, rp):
             a_codes[kp, rp] = keep.tile([P, PASS], U32, name="a_codes%d%d" % (kp, rp), align_bytes=64)
@@ -135,7 +142,7 @@ def tile_list_click_feature_grad_kernel(
             nc.vector.quantize_mx(a_codes[kp, rp][:].bitcast(FP8X4), a_planes[kp, rp][:], a_round[kp, rp][:])
 
         for rp in range(R_PASSES):
-            round_a(0, rp, slice(0, PACK), nc.scalar.copy if rp == LAST else nc.vector.tensor_copy)
+            round_a(0, rp)
         for rp in range(R_PASSES):
             quantise_a(0, rp)
 
@@ -144,18 +151,18 @@ def tile_list_click_feature_grad_kernel(
             nc.vector.tensor_copy(v_codes[kp][:], tab[kp][:].bitcast(U32).indirect(offsets[:]))
         v_planes = keep.tile([P, S], U8, name="v_planes", tag="tab0", align_bytes=64)
         nc.vector.tensor_copy(v_planes[:], tab_scale_rows[:].indirect(offsets[:]))
-        wb_planes = keep.tile([P, R_PASSES, N], U8, name="wb_planes", tag="tab1", align_bytes=64)
+        wb_planes = keep.tile([P, LAST, N], U8, name="wb_planes", tag="tab1", align_bytes=64)
         nc.vector.tensor_copy(
             wb_planes[:].rearrange("p rp (g t m) -> p (rp g) t m", g=N_GROUPS, t=PACK),
             wb_scale_rows[:].rearrange("p rp (g m t) -> p (rp g) t m", g=N_GROUPS, t=PACK),
         )
 
-        load_labels(6)
+        load_labels(LABEL_PLACES)
         for rp in range(R_PASSES):
-            round_a(1, rp, slice(0, PACK), nc.scalar.copy if rp == LAST else nc.vector.tensor_copy)
+            round_a(1, rp)
         for rp in range(R_PASSES):
             quantise_a(1, rp)
-        load_labels(7)
+        load_labels(LABEL_PLACES + 1)
 
         for rp in range(R_PASSES):
             for t in range(PACK):
@@ -191,7 +198,7 @@ def tile_list_click_feature_grad_kernel(
         def row_gradient(rp, t):
             scale = minus_weight[:, t, rp : rp + 1]
             miss = ring.tile([P, S], F32, name="miss", bufs=MISS_BUFS)
-            pieces = {(LAST, PACK - 1): (slice(0, 64), slice(64, 128)) + QUARTERS[1:], (LAST, PACK - 2): QUARTERS, (LAST, PACK - 3): HALVES, (LAST, 0): HALVES}.get((rp, t), WHOLE)
+            pieces = LAST_PIECES[t] if rp == LAST else WHOLE
             for cols in pieces:
                 picked = label_rows[rp, t][:].indirect(offsets[:, cols.start // 16 : cols.stop // 16])
                 part = prob[rp, t, cols.start][:] if (rp, t) == (LAST, 0) else prob[rp, t, 0][:, cols]
@@ -200,41 +207,49 @@ def tile_list_click_feature_grad_kernel(
                 place = d_round[rp][:, cols, t] if rp == LAST else d_pairs[rp][:, t // 2, cols, t % 2]
                 nc.scalar.activation(place, miss[:, cols], ACT.Copy, scale=scale)
 
-        d_codes, d_plane, last_raw = {}, {}, []
+        d_codes, d_plane, late_raw = {}, {}, {}
+        wb_plane = {rp: wb_planes[:, rp, :] for rp in range(LAST)}
 
         def load_last_words():
-            last_raw.append(keep.tile([P, 2 * N], U8, name="last_raw", tag="prob10", align_bytes=64))
-            nc.sync.dma_start(last_raw[0][:].bitcast(I32), wb_words[LAST].bitcast(I32))
+            late_raw[LAST] = keep.tile([P, 2 * N], U8, name="late_raw", tag="prob10", align_bytes=64)
+            nc.sync.dma_start(late_raw[LAST][:].bitcast(I32), wb_words[LAST].bitcast(I32))
+            last_plane = keep.tile([P, N], U8, name="last_plane", tag="prob11", align_bytes=64)
+            for quad in range(QUADS):
+                nc.sync.dma_start(
+                    last_plane[32 * quad : 32 * quad + QUAD_ROWS, :].bitcast(I32),
+                    wb_planes[32 * quad + QUAD_ROWS : 32 * (quad + 1) : PARK_STEP, 0, :].bitcast(I32),
+                )
+            wb_plane[LAST] = last_plane[:]
 
         def quantise_d(rp, after):
             d_codes[rp] = keep.tile([P, S], U32, name="d_codes", tag="prob%d%d" % after, align_bytes=64)
             d_plane[rp] = keep.tile([P, S], U8, name="d_plane%d" % rp, align_bytes=64)
             for piece, cols in enumerate(QUARTERS if rp == LAST else WHOLE):
                 if rp == LAST and piece % 2 == 0:
-                    deal_words(LAST, last_raw[0][:], piece, 2, "last_codes%d" % piece)
+                    deal_words(LAST, late_raw[LAST][:], piece, 2, "last_codes%d" % piece)
                 nc.vector.quantize_mx(
                     d_codes[rp][:, cols].bitcast(FP8X4),
                     d_plane[rp][:, cols],
                     d_round[rp][:, cols, :].rearrange("p j t -> p (j t)"),
                 )
             if rp == LAST:
-                deal_words(LAST, last_raw[0][:], PACK, PACK, "d_round%d" % LAST)
+                deal_words(LAST, late_raw[LAST][:], PACK, PACK, "d_round%d" % LAST)
 
-        def back_project(rp, banks):
+        def back_project(rp, groups):
             first = rp == 0
 
             def one_pass(out, rows_no, cols, start, stop):
                 nc.tensor.matmul_mx(
                     out,
                     lhsT=wb_codes[rp, rows_no].bitcast(FP4X4),
-                    lhsT_scale=wb_planes[:, rp, P * rows_no : P * (rows_no + 1)],
+                    lhsT_scale=wb_plane[rp][:, P * rows_no : P * (rows_no + 1)],
                     rhs=d_codes[rp][:, cols].bitcast(FP8X4),
                     rhs_scale=d_plane[rp][:, cols],
                     start=start,
                     stop=stop,
                 )
 
-            for half in range(2 if 0 in banks else 0):
+            for half in range(2 if 0 in groups else 0):
                 for pair in range(2):
                     for q in range(2):
                         for row in range(2):
@@ -246,27 +261,27 @@ def tile_list_click_feature_grad_kernel(
                                 first and q == 0 and row == 0,
                                 rp == LAST and q == 1 and row == 1,
                             )
-            for bank_no in range(max(PACK, banks.start), banks.stop):
+            for bank_no in range(PACK, PSUM_BANKS if 1 in groups else PACK):
                 one_pass(y_banks[bank_no][:], bank_no, WHOLE[0], first, rp == LAST)
 
         closing = {0: 0, 1: 1, 3: LAST}
-        for step, (rp, t, count) in enumerate(loads):
+        for step, (rp, t) in enumerate(loads):
             row_gradient(rp, t)
-            if step < 4:
-                load_labels(8 + step)
-            if step == 4:
+            if step + len(first_places) < len(loads):
+                load_labels(step + len(first_places))
+            if (rp, t) == (1, 1):
                 load_last_words()
-            if rp < LAST and t + count == PACK:
+            if rp < LAST and t == PACK - 1:
                 weave(rp)
             if rp == LAST and t in closing:
                 quantise_d(closing[t], (rp, t))
-                back_project(closing[t], range(PACK if t == 1 else PSUM_BANKS))
+                back_project(closing[t], (0,) if t == 1 else (0, 1))
             if (rp, t) == (LAST, 2):
                 deal_words(1, wb_raw[:, 1, :], PACK, PACK, "prob%d%d" % (rp, t))
-                back_project(1, range(PACK, PSUM_BANKS))
+                back_project(1, (1,))
 
         y_planes = keep.tile([P, N_GROUPS, S], U8, name="y_planes", align_bytes=64)
-        y, y_round, early = [], [], []
+        y, y_round, y_early = [], [], []
 
         def empty_banks(g):
             y.append(keep.tile([P, PACK, S], F32, name="y", tag="wide%d" % g, align_bytes=64))
@@ -291,16 +306,17 @@ def tile_list_click_feature_grad_kernel(
 
         def round_y(g):
             y_round.append(ring.tile([P, S, PACK], BF16, name="y_round", tag="round", bufs=ROUND_BUFS, align_bytes=64))
-            split = S if g == 0 else S // 4
+            split = S if g == 0 else VECTOR_ROUNDS
             first = HALF if g == 0 else 0
             if g == 0:
-                early.append(keep.tile([P, HALF, PACK], BF16, name="y_early", tag="prob10", align_bytes=64))
-                nc.gpsimd.tensor_scalar(early[0][:], y[g][:, :, :HALF].rearrange("p t j -> p j t"), 1.0, 0.0, ALU.mult, ALU.add)
+                y_early.append(keep.tile([P, HALF, PACK], BF16, name="y_early", tag="prob10", align_bytes=64))
+                columns = y[g][:, :, :HALF].rearrange("p t j -> p j t")
+                nc.gpsimd.tensor_scalar(y_early[0][:], columns, 1.0, 0.0, ALU.mult, ALU.add)
             nc.vector.tensor_copy(
                 y_round[g][:, first:split, :].rearrange("p (run near) t -> p run t near", near=NEAR),
                 y[g][:, :, first:split].rearrange("p t (run near) -> p run t near", near=NEAR),
             )
-            for cols in () if g == 0 else QUARTERS[1:]:
+            for cols in () if g == 0 else QUARTERS[VECTOR_ROUNDS // P :]:
                 nc.scalar.copy(
                     y_round[g][:, cols, :].rearrange("p (run near) t -> p run t near", near=NEAR),
                     y[g][:, :, cols].rearrange("p t (run near) -> p run t near", near=NEAR),
@@ -310,10 +326,11 @@ def tile_list_click_feature_grad_kernel(
             y_codes = keep.tile([P, S], U32, name="y_codes%d" % g, align_bytes=64)
             words = out_1[g].rearrange("p j t -> p (j t)").bitcast(I32)
             for cols in HALVES if g == 0 else (HALVES[0],) + QUARTERS[2:]:
+                rounded = y_early[0][:] if (g, cols.start) == (0, 0) else y_round[g][:, cols, :]
                 nc.vector.quantize_mx(
                     y_codes[:, cols].bitcast(FP8X4),
                     y_planes[:, g, cols],
-                    (early[0][:] if (g, cols.start) == (0, 0) else y_round[g][:, cols, :]).rearrange("p j t -> p (j t)"),
+                    rounded.rearrange("p j t -> p (j t)"),
                 )
             nc.sync.dma_start(words, y_codes[:].bitcast(I32))
 

@@ -57,13 +57,11 @@ def tile_list_click_feature_grad_kernel(
         wb_scale_rows = keep.tile([P, LAST, N], U8, name="wb_scale_rows", align_bytes=64)
         slot_rows = keep.tile([P, PASS], F32, name="slot_rows")
         identity = keep.tile([P, P], F32, name="identity")
-        nc.gpsimd.memset(slot_rows[:], 0.0)
         make_identity(nc, identity[:])
         nc.vector.memset(tab_scale_rows[:].bitcast(I32), 0)
         nc.vector.memset(wb_scale_rows[:].bitcast(I32), 0)
+        nc.vector.memset(slot_rows[:], 0.0)
 
-        nc.scalar.dma_start(slot_rows[BIAS_ROWS, :], b.rearrange("(rp r) -> rp r", r=PASS))
-        nc.scalar.dma_start(slot_rows[WEIGHT_ROWS, :], c.rearrange("(rp r) -> rp r", r=PASS))
         for quad in range(QUADS):
             nc.gpsimd.dma_start(
                 tab_scale_rows[32 * quad + QUAD_ROWS : 32 * quad + QUAD_ROWS * (1 + K_PASSES), :].bitcast(I32),
@@ -74,6 +72,8 @@ def tile_list_click_feature_grad_kernel(
                 wb_scale_rows[row:P:32, :, :].bitcast(I32),
                 wb_scales[:LAST, row::QUAD_ROWS, :].rearrange("rp quad n -> quad rp n").bitcast(I32),
             )
+        nc.scalar.dma_start(slot_rows[BIAS_ROWS, :], b.rearrange("(rp r) -> rp r", r=PASS))
+        nc.scalar.dma_start(slot_rows[WEIGHT_ROWS, :], c.rearrange("(rp r) -> rp r", r=PASS))
         nc.gpsimd.dma_start(wb_scale_rows[QUAD_ROWS:P:PARK_STEP, 0, :].bitcast(I32), wb_scales[LAST].bitcast(I32))
 
         wb_raw = keep.tile([P, LAST, 2 * N], U8, name="wb_raw", align_bytes=64)

@@ -37,7 +37,7 @@ NEAR = 4
 PSUM_BANKS = 8
 ROUND_BUFS = R_PASSES
 MISS_BUFS = 6
-LABEL_PLACES = 6
+PAIRS = 3
 VECTOR_ROUNDS = S // 4
 BIAS_ROWS, WEIGHT_ROWS = slice(12, 24, 4), slice(76, 88, 4)
 
@@ -82,24 +82,24 @@ def tile_list_click_feature_grad_kernel(
         a_raw = [keep.tile([P, PACK, H], F32, name="a_raw", tag="wide%d" % kp, align_bytes=64) for kp in range(K_PASSES)]
         tab = [keep.tile([P, T], I32, name="tab%d" % kp, align_bytes=64) for kp in range(K_PASSES)]
         a_rows = a.rearrange("(kp p i) r -> kp p i r", p=P, i=PACK)
-        nc.sync.dma_start(a_raw[0][:], a_rows[0])
         for kp in range(K_PASSES):
+            nc.sync.dma_start(a_raw[kp][:], a_rows[kp])
             nc.sync.dma_start(tab[kp][:], tab_words[kp].rearrange("p x i -> p (x i)").bitcast(I32))
-        nc.sync.dma_start(a_raw[1][:], a_rows[1])
 
         loads = [(rp, t) for rp in range(R_PASSES) for t in range(PACK)]
-        own_places = ["label%d" % k for k in range(LABEL_PLACES)]
-        first_places = own_places + ["wide%d" % kp for kp in range(K_PASSES)]
-        places = (first_places + own_places)[: len(loads)]
+        pair_places = ["label%d" % k for k in range(PAIRS)]
+        single_places = ["wide0", "wide1", "label0", "label1", "prob03", "label2"]
         label_rows = {}
 
         def load_labels(step):
             rp, t = loads[step]
-            label_rows[rp, t] = keep.tile([P, T], F32, name="label_rows", tag=places[step], align_bytes=64)
+            count = 2 if step < 2 * PAIRS else 1
+            place = pair_places[step // 2] if count == 2 else single_places[step - 2 * PAIRS]
+            label_rows[rp, t] = keep.tile([P, count * T], F32, name="label_rows", tag=place, align_bytes=64)
             rows = gT[rp * PASS : (rp + 1) * PASS, :].rearrange("(p t) x -> p (t x)", t=PACK)
-            nc.sync.dma_start(label_rows[rp, t][:], rows[:, t * T : (t + 1) * T])
+            nc.sync.dma_start(label_rows[rp, t][:], rows[:, t * T : (t + count) * T])
 
-        for step in range(LABEL_PLACES):
+        for step in range(0, 2 * PAIRS, 2):
             load_labels(step)
 
         wb_codes = {}
@@ -157,12 +157,12 @@ def tile_list_click_feature_grad_kernel(
             wb_scale_rows[:].rearrange("p rp (g m t) -> p (rp g) t m", g=N_GROUPS, t=PACK),
         )
 
-        load_labels(LABEL_PLACES)
+        load_labels(2 * PAIRS)
         for rp in range(R_PASSES):
             round_a(1, rp)
         for rp in range(R_PASSES):
             quantise_a(1, rp)
-        load_labels(LABEL_PLACES + 1)
+        load_labels(2 * PAIRS + 1)
 
         for rp in range(R_PASSES):
             for t in range(PACK):
@@ -199,7 +199,11 @@ def tile_list_click_feature_grad_kernel(
             scale = minus_weight[:, t, rp : rp + 1]
             miss = ring.tile([P, S], F32, name="miss", bufs=MISS_BUFS)
             pieces = LAST_PIECES[t] if rp == LAST else WHOLE
-            for cols in pieces:
+            if (rp, t) not in label_rows:
+                second = ring.tile([P, S], F32, name="second")
+                nc.vector.tensor_copy(second[:], label_rows[rp, t - 1][:, T:].indirect(offsets[:]))
+                nc.vector.tensor_tensor(miss[:], second[:], prob[rp, t, 0][:], ALU.subtract)
+            for cols in pieces if (rp, t) in label_rows else ():
                 picked = label_rows[rp, t][:].indirect(offsets[:, cols.start // 16 : cols.stop // 16])
                 part = prob[rp, t, cols.start][:] if (rp, t) == (LAST, 0) else prob[rp, t, 0][:, cols]
                 nc.vector.tensor_tensor(miss[:, cols], picked, part, ALU.subtract)
@@ -211,9 +215,9 @@ def tile_list_click_feature_grad_kernel(
         wb_plane = {rp: wb_planes[:, rp, :] for rp in range(LAST)}
 
         def load_last_words():
-            late_raw[LAST] = keep.tile([P, 2 * N], U8, name="late_raw", tag="prob10", align_bytes=64)
+            late_raw[LAST] = keep.tile([P, 2 * N], U8, name="late_raw", tag="prob12", align_bytes=64)
             nc.sync.dma_start(late_raw[LAST][:].bitcast(I32), wb_words[LAST].bitcast(I32))
-            last_plane = keep.tile([P, N], U8, name="last_plane", tag="prob11", align_bytes=64)
+            last_plane = keep.tile([P, N], U8, name="last_plane", tag="prob13", align_bytes=64)
             for quad in range(QUADS):
                 nc.sync.dma_start(
                     last_plane[32 * quad : 32 * quad + QUAD_ROWS, :].bitcast(I32),
@@ -267,9 +271,9 @@ def tile_list_click_feature_grad_kernel(
         closing = {0: 0, 1: 1, 3: LAST}
         for step, (rp, t) in enumerate(loads):
             row_gradient(rp, t)
-            if step + len(first_places) < len(loads):
-                load_labels(step + len(first_places))
-            if (rp, t) == (1, 1):
+            for later in {1: (8,), 3: (9, 10), 5: (11,)}.get(step, ()):
+                load_labels(later)
+            if (rp, t) == (1, 3):
                 load_last_words()
             if rp < LAST and t == PACK - 1:
                 weave(rp)
@@ -309,7 +313,7 @@ def tile_list_click_feature_grad_kernel(
             split = S if g == 0 else VECTOR_ROUNDS
             first = HALF if g == 0 else 0
             if g == 0:
-                y_early.append(keep.tile([P, HALF, PACK], BF16, name="y_early", tag="prob10", align_bytes=64))
+                y_early.append(keep.tile([P, HALF, PACK], BF16, name="y_early", tag="prob12", align_bytes=64))
                 columns = y[g][:, :, :HALF].rearrange("p t j -> p j t")
                 nc.gpsimd.tensor_scalar(y_early[0][:], columns, 1.0, 0.0, ALU.mult, ALU.add)
             nc.vector.tensor_copy(

@@ -37,7 +37,7 @@ NEAR = 4
 PSUM_BANKS = 8
 ROUND_BUFS = R_PASSES
 MISS_BUFS = 6
-PAIRS = 3
+PAIRS = 2
 VECTOR_ROUNDS = S // 4
 BIAS_ROWS, WEIGHT_ROWS = slice(12, 24, 4), slice(76, 88, 4)
 
@@ -88,7 +88,7 @@ def tile_list_click_feature_grad_kernel(
 
         loads = [(rp, t) for rp in range(R_PASSES) for t in range(PACK)]
         pair_places = ["label%d" % k for k in range(PAIRS)]
-        single_places = ["wide0", "wide1", "label0", "label1", "prob03", "label2"]
+        single_places = ["label2", "label3", "wide0", "wide1", "label0", "prob01", "label1", "label2"]
         label_rows = {}
 
         def load_labels(step):
@@ -99,7 +99,7 @@ def tile_list_click_feature_grad_kernel(
             rows = gT[rp * PASS : (rp + 1) * PASS, :].rearrange("(p t) x -> p (t x)", t=PACK)
             nc.sync.dma_start(label_rows[rp, t][:], rows[:, t * T : (t + count) * T])
 
-        for step in range(0, 2 * PAIRS, 2):
+        for step in (0, 2, 4, 5):
             load_labels(step)
 
         wb_codes = {}
@@ -115,8 +115,9 @@ def tile_list_click_feature_grad_kernel(
             for k in range(count):
                 wb_codes[rp, rows_no + k] = dealt[:, k, :]
 
-        for rp, g in ((0, 0), (0, 1), (1, 0)):
-            deal_words(rp, wb_raw[:, rp, :], g * PACK, PACK, "wb_codes%d%d" % (rp, g))
+        for rp in range(LAST):
+            for g in range(N_GROUPS):
+                deal_words(rp, wb_raw[:, rp, :], g * PACK, PACK, "wb_codes%d%d" % (rp, g))
 
         turned = psum.tile([P, PACK, P], F32, name="bank")
         for t in range(PACK):
@@ -151,18 +152,18 @@ def tile_list_click_feature_grad_kernel(
             nc.vector.tensor_copy(v_codes[kp][:], tab[kp][:].bitcast(U32).indirect(offsets[:]))
         v_planes = keep.tile([P, S], U8, name="v_planes", tag="tab0", align_bytes=64)
         nc.vector.tensor_copy(v_planes[:], tab_scale_rows[:].indirect(offsets[:]))
-        wb_planes = keep.tile([P, LAST, N], U8, name="wb_planes", tag="tab1", align_bytes=64)
+        wb_planes = keep.tile([P, LAST, N], U8, name="wb_planes", tag="tab_scale_rows", align_bytes=64)
         nc.vector.tensor_copy(
             wb_planes[:].rearrange("p rp (g t m) -> p (rp g) t m", g=N_GROUPS, t=PACK),
             wb_scale_rows[:].rearrange("p rp (g m t) -> p (rp g) t m", g=N_GROUPS, t=PACK),
         )
 
-        load_labels(2 * PAIRS)
+        load_labels(6)
         for rp in range(R_PASSES):
             round_a(1, rp)
         for rp in range(R_PASSES):
             quantise_a(1, rp)
-        load_labels(2 * PAIRS + 1)
+        load_labels(7)
 
         for rp in range(R_PASSES):
             for t in range(PACK):
@@ -195,14 +196,17 @@ def tile_list_click_feature_grad_kernel(
                 d_pairs[rp][:].rearrange("p u j e -> p (u j e)").bitcast(U32).rearrange("p (u j) -> p j u", u=2),
             )
 
+        second = {}
+
         def row_gradient(rp, t):
             scale = minus_weight[:, t, rp : rp + 1]
             miss = ring.tile([P, S], F32, name="miss", bufs=MISS_BUFS)
             pieces = LAST_PIECES[t] if rp == LAST else WHOLE
-            if (rp, t) not in label_rows:
-                second = ring.tile([P, S], F32, name="second")
-                nc.vector.tensor_copy(second[:], label_rows[rp, t - 1][:, T:].indirect(offsets[:]))
-                nc.vector.tensor_tensor(miss[:], second[:], prob[rp, t, 0][:], ALU.subtract)
+            if (rp, t + 1) in loads[1 : 2 * PAIRS : 2]:
+                second[rp, t + 1] = ring.tile([P, S], F32, name="second")
+                nc.vector.tensor_copy(second[rp, t + 1][:], label_rows[rp, t][:, T:].indirect(offsets[:]))
+            if (rp, t) in second:
+                nc.vector.tensor_tensor(miss[:], second[rp, t][:], prob[rp, t, 0][:], ALU.subtract)
             for cols in pieces if (rp, t) in label_rows else ():
                 picked = label_rows[rp, t][:].indirect(offsets[:, cols.start // 16 : cols.stop // 16])
                 part = prob[rp, t, cols.start][:] if (rp, t) == (LAST, 0) else prob[rp, t, 0][:, cols]
@@ -215,7 +219,7 @@ def tile_list_click_feature_grad_kernel(
         wb_plane = {rp: wb_planes[:, rp, :] for rp in range(LAST)}
 
         def load_last_words():
-            late_raw[LAST] = keep.tile([P, 2 * N], U8, name="late_raw", tag="prob12", align_bytes=64)
+            late_raw[LAST] = keep.tile([P, 2 * N], U8, name="late_raw", tag="prob11", align_bytes=64)
             nc.sync.dma_start(late_raw[LAST][:].bitcast(I32), wb_words[LAST].bitcast(I32))
             last_plane = keep.tile([P, N], U8, name="last_plane", tag="prob13", align_bytes=64)
             for quad in range(QUADS):
@@ -225,38 +229,42 @@ def tile_list_click_feature_grad_kernel(
                 )
             wb_plane[LAST] = last_plane[:]
 
-        def quantise_d(rp, after):
-            d_codes[rp] = keep.tile([P, S], U32, name="d_codes", tag="prob%d%d" % after, align_bytes=64)
-            d_plane[rp] = keep.tile([P, S], U8, name="d_plane%d" % rp, align_bytes=64)
-            for piece, cols in enumerate(QUARTERS if rp == LAST else WHOLE):
+        def quantise_d(rp, span, after):
+            codes = keep.tile([P, span.stop - span.start], U32, name="d_codes", tag="prob%d%d" % after, align_bytes=64)
+            for q in range(span.start // P, span.stop // P):
+                d_codes[rp, q] = (codes, span.start)
+            if span.start == 0:
+                d_plane[rp] = keep.tile([P, S], U8, name="d_plane%d" % rp, align_bytes=64)
+            for piece, cols in enumerate(QUARTERS if rp == LAST else (span,)):
                 if rp == LAST and piece % 2 == 0:
                     deal_words(LAST, late_raw[LAST][:], piece, 2, "last_codes%d" % piece)
                 nc.vector.quantize_mx(
-                    d_codes[rp][:, cols].bitcast(FP8X4),
+                    codes[:, cols.start - span.start : cols.stop - span.start].bitcast(FP8X4),
                     d_plane[rp][:, cols],
                     d_round[rp][:, cols, :].rearrange("p j t -> p (j t)"),
                 )
             if rp == LAST:
                 deal_words(LAST, late_raw[LAST][:], PACK, PACK, "d_round%d" % LAST)
 
-        def back_project(rp, groups):
+        def back_project(rp, span):
             first = rp == 0
 
             def one_pass(out, rows_no, cols, start, stop):
+                codes, begin = d_codes[rp, cols.start // P]
                 nc.tensor.matmul_mx(
                     out,
                     lhsT=wb_codes[rp, rows_no].bitcast(FP4X4),
                     lhsT_scale=wb_plane[rp][:, P * rows_no : P * (rows_no + 1)],
-                    rhs=d_codes[rp][:, cols].bitcast(FP8X4),
+                    rhs=codes[:, cols.start - begin : cols.stop - begin].bitcast(FP8X4),
                     rhs_scale=d_plane[rp][:, cols],
                     start=start,
                     stop=stop,
                 )
 
-            for half in range(2 if 0 in groups else 0):
+            for half in range(2):
                 for pair in range(2):
                     for q in range(2):
-                        for row in range(2):
+                        for row in range(2 if span.start <= QUARTERS[2 * half + q].start < span.stop else 0):
                             place = row * HALF + q * P
                             one_pass(
                                 y_banks[2 * half + pair][:, place : place + P],
@@ -265,24 +273,22 @@ def tile_list_click_feature_grad_kernel(
                                 first and q == 0 and row == 0,
                                 rp == LAST and q == 1 and row == 1,
                             )
-            for bank_no in range(PACK, PSUM_BANKS if 1 in groups else PACK):
-                one_pass(y_banks[bank_no][:], bank_no, WHOLE[0], first, rp == LAST)
+            for bank_no in range(PACK, PSUM_BANKS):
+                for cols in {S: WHOLE, 3 * P: (HALVES[0], QUARTERS[2]), P: QUARTERS[3:]}[span.stop - span.start]:
+                    one_pass(y_banks[bank_no][:, cols], bank_no, cols, first, rp == LAST)
 
-        closing = {0: 0, 1: 1, 3: LAST}
+        closing = {(1, 2): (0, WHOLE[0]), (LAST, 1): (1, slice(0, 3 * P)), (LAST, 2): (1, QUARTERS[3]), (LAST, 3): (LAST, WHOLE[0])}
         for step, (rp, t) in enumerate(loads):
             row_gradient(rp, t)
-            for later in {1: (8,), 3: (9, 10), 5: (11,)}.get(step, ()):
+            for later in {0: (8,), 1: (9,), 2: (10,), 4: (11,)}.get(step, ()):
                 load_labels(later)
             if (rp, t) == (1, 3):
                 load_last_words()
             if rp < LAST and t == PACK - 1:
                 weave(rp)
-            if rp == LAST and t in closing:
-                quantise_d(closing[t], (rp, t))
-                back_project(closing[t], (0,) if t == 1 else (0, 1))
-            if (rp, t) == (LAST, 2):
-                deal_words(1, wb_raw[:, 1, :], PACK, PACK, "prob%d%d" % (rp, t))
-                back_project(1, (1,))
+            if (rp, t) in closing:
+                quantise_d(*closing[rp, t], (rp, t))
+                back_project(*closing[rp, t])
 
         y_planes = keep.tile([P, N_GROUPS, S], U8, name="y_planes", align_bytes=64)
         y, y_round, y_early = [], [], []
@@ -313,7 +319,7 @@ def tile_list_click_feature_grad_kernel(
             split = S if g == 0 else VECTOR_ROUNDS
             first = HALF if g == 0 else 0
             if g == 0:
-                y_early.append(keep.tile([P, HALF, PACK], BF16, name="y_early", tag="prob12", align_bytes=64))
+                y_early.append(keep.tile([P, HALF, PACK], BF16, name="y_early", tag="prob11", align_bytes=64))
                 columns = y[g][:, :, :HALF].rearrange("p t j -> p j t")
                 nc.gpsimd.tensor_scalar(y_early[0][:], columns, 1.0, 0.0, ALU.mult, ALU.add)
             nc.vector.tensor_copy(

from contextlib import ExitStack

import concourse.mybir as mybir
from concourse.masks import make_identity

K, N, H, T, S = 1024, 1024, 1536, 2048, 512
FLOPS = 2 * K * H * S + 2 * H * N * S

F32 = mybir.dt.float32
BF16 = mybir.dt.bfloat16
I32 = mybir.dt.int32
U32 = mybir.dt.uint32
U16 = mybir.dt.uint16
U8 = mybir.dt.uint8
FP8X4 = mybir.dt.float8_e4m3fn_x4
FP4X4 = mybir.dt.float4_e2m1fn_x4
ALU = mybir.AluOpType
ACT = mybir.ActivationFunctionType

P = 128
PACK = 4
PASS = P * PACK
QUADS = 4
QUAD_ROWS = 4
K_PASSES = K // PASS
R_PASSES = H // PASS
N_GROUPS = N // PASS
LAST = R_PASSES - 1
HALF = S // 2
HALVES = (slice(0, HALF), slice(HALF, S))
QUARTERS = tuple(slice(q * S // 4, (q + 1) * S // 4) for q in range(4))
EIGHTHS = (slice(0, S // 8), slice(S // 8, S // 4))
WHOLE = (slice(0, S),)
LAST_PIECES = (HALVES, HALVES, QUARTERS, EIGHTHS + QUARTERS[1:])
PARK_STEP = 8
NEAR = 4
PSUM_BANKS = 8
ROUND_BUFS = R_PASSES
MISS_BUFS = 6
PAIRS = 2
VECTOR_ROUNDS = S // 4
BIAS_ROWS, WEIGHT_ROWS = slice(12, 24, 4), slice(76, 88, 4)


def tile_list_click_feature_grad_kernel(
    tc, tab_words, tab_scales, offs, a, b, gT, c, wb_words, wb_scales, out_0, out_1, out_2
):
    nc = tc.nc
    with ExitStack() as ctx:
        keep = ctx.enter_context(tc.tile_pool(name="keep", bufs=1))
        ring = ctx.enter_context(tc.tile_pool(name="ring", bufs=2))
        psum = ctx.enter_context(tc.psum_pool(name="psum", bufs=PSUM_BANKS))

        offsets = keep.tile([P, S // 16], U16, name="offsets")

        tab_scale_rows = keep.tile([P, T], U8, name="tab_scale_rows", align_bytes=64)
        wb_scale_rows = keep.tile([P, LAST, N], U8, name="wb_scale_rows", align_bytes=64)
        slot_rows = keep.tile([P, PASS], F32, name="slot_rows")
        identity = keep.tile([P, P], F32, name="identity")
        make_identity(nc, identity[:])
        nc.vector.memset(tab_scale_rows[:].bitcast(I32), 0)
        nc.vector.memset(wb_scale_rows[:].bitcast(I32), 0)
        nc.vector.memset(slot_rows[:], 0.0)

        for quad in range(QUADS):
            nc.gpsimd.dma_start(
                tab_scale_rows[32 * quad + QUAD_ROWS : 32 * quad + QUAD_ROWS * (1 + K_PASSES), :].bitcast(I32),
                tab_scales[:, QUAD_ROWS * quad : QUAD_ROWS * (quad + 1), :].bitcast(I32),
            )
        for row in range(QUAD_ROWS):
            nc.scalar.dma_start(
                wb_scale_rows[row:P:32, :, :].bitcast(I32),
                wb_scales[:LAST, row::QUAD_ROWS, :].rearrange("rp quad n -> quad rp n").bitcast(I32),
            )
        nc.scalar.dma_start(slot_rows[BIAS_ROWS, :], b.rearrange("(rp r) -> rp r", r=PASS))
        nc.scalar.dma_start(slot_rows[WEIGHT_ROWS, :], c.rearrange("(rp r) -> rp r", r=PASS))
        nc.gpsimd.dma_start(wb_scale_rows[QUAD_ROWS:P:PARK_STEP, 0, :].bitcast(I32), wb_scales[LAST].bitcast(I32))

        wb_raw = keep.tile([P, LAST, 2 * N], U8, name="wb_raw", align_bytes=64)
        nc.sync.dma_start(wb_raw[:].bitcast(I32), wb_words[:LAST].rearrange("rp p w -> p rp w").bitcast(I32))
        nc.sync.dma_start(offsets[:], offs)
        a_raw = [keep.tile([P, PACK, H], F32, name="a_raw", tag="wide%d" % kp, align_bytes=64) for kp in range(K_PASSES)]
        tab = [keep.tile([P, T], I32, name="tab%d" % kp, align_bytes=64) for kp in range(K_PASSES)]
        a_rows = a.rearrange("(kp p i) r -> kp p i r", p=P, i=PACK)
        for kp in range(K_PASSES):
            nc.sync.dma_start(a_raw[kp][:], a_rows[kp])
            nc.sync.dma_start(tab[kp][:], tab_words[kp].rearrange("p x i -> p (x i)").bitcast(I32))

        loads = [(rp, t) for rp in range(R_PASSES) for t in range(PACK)]
        pair_places = ["label%d" % k for k in range(PAIRS)]
        single_places = ["label2", "label3", "wide0", "wide1", "label0", "prob01", "label1", "label2"]
        label_rows = {}

        def load_labels(step):
            rp, t = loads[step]
            count = 2 if step < 2 * PAIRS else 1
            place = pair_places[step // 2] if count == 2 else single_places[step - 2 * PAIRS]
            label_rows[rp, t] = keep.tile([P, count * T], F32, name="label_rows", tag=place, align_bytes=64)
            rows = gT[rp * PASS : (rp + 1) * PASS, :].rearrange("(p t) x -> p (t x)", t=PACK)
            nc.sync.dma_start(label_rows[rp, t][:], rows[:, t * T : (t + count) * T])

        for step in (0, 2, 4, 5):
            load_labels(step)

        wb_codes = {}

        def deal_words(rp, raw, rows_no, count, tag):
            dealt = keep.tile([P, count, 2 * P], U8, name="wb_dealt", tag=tag, align_bytes=64)
            g, t = divmod(rows_no, PACK)
            words = raw.bitcast(U16).rearrange("p (g m t) -> p g t m", g=N_GROUPS, t=PACK)
            nc.vector.tensor_copy(
                dealt[:].rearrange("p t w -> p (t w)").bitcast(U16).rearrange("p (t m) -> p t m", t=count),
                words[:, g, t : t + count, :],
            )
            for k in range(count):
                wb_codes[rp, rows_no + k] = dealt[:, k, :]

        for rp in range(LAST):
            for g in range(N_GROUPS):
                deal_words(rp, wb_raw[:, rp, :], g * PACK, PACK, "wb_codes%d%d" % (rp, g))

        turned = psum.tile([P, PACK, P], F32, name="bank")
        for t in range(PACK):
            nc.tensor.transpose(turned[:, t, :], slot_rows[:, t::PACK], identity[:])
        bias = keep.tile([P, PACK, R_PASSES], F32, name="bias")
        minus_weight = keep.tile([P, PACK, R_PASSES], F32, name="minus_weight")
        nc.scalar.copy(bias[:], turned[:, :, BIAS_ROWS])
        nc.scalar.activation(minus_weight[:], turned[:, :, WEIGHT_ROWS], ACT.Copy, scale=-1.0)

        a_round, a_codes, a_planes, prob = {}, {}, {}, {}

        def round_a(kp, rp):
            engine_copy = nc.scalar.copy if rp == LAST else nc.vector.tensor_copy
            a_round[kp, rp] = ring.tile([P, PACK * PASS], BF16, name="a_round", tag="round", bufs=ROUND_BUFS, align_bytes=64)
            dealt = a_round[kp, rp][:].rearrange("p (u e m i) -> p u m i e", u=2, e=2, i=PACK)
            block = a_raw[kp][:, :, rp * PASS : (rp + 1) * PASS].rearrange("p i (m u e) -> p u m i e", u=2, e=2)
            for u in range(2):
                engine_copy(dealt[:, u, :, :, :], block[:, u, :, :, :])

        def quantise_a(kp, rp):
            a_codes[kp, rp] = keep.tile([P, PASS], U32, name="a_codes%d%d" % (kp, rp), align_bytes=64)
            a_planes[kp, rp] = keep.tile([P, PASS], U8, name="a_planes%d%d" % (kp, rp), align_bytes=64)
            nc.vector.quantize_mx(a_codes[kp, rp][:].bitcast(FP8X4), a_planes[kp, rp][:], a_round[kp, rp][:])

        for rp in range(R_PASSES):
            round_a(0, rp)
        for rp in range(R_PASSES):
            quantise_a(0, rp)

        v_codes = [keep.tile([P, S], U32, name="v_codes%d" % kp, align_bytes=64) for kp in range(K_PASSES)]
        for kp in range(K_PASSES):
            nc.vector.tensor_copy(v_codes[kp][:], tab[kp][:].bitcast(U32).indirect(offsets[:]))
        v_planes = keep.tile([P, S], U8, name="v_planes", tag="tab0", align_bytes=64)
        nc.vector.tensor_copy(v_planes[:], tab_scale_rows[:].indirect(offsets[:]))
        wb_planes = keep.tile([P, LAST, N], U8, name="wb_planes", tag="tab_scale_rows", align_bytes=64)
        nc.vector.tensor_copy(
            wb_planes[:].rearrange("p rp (g t m) -> p (rp g) t m", g=N_GROUPS, t=PACK),
            wb_scale_rows[:].rearrange("p rp (g m t) -> p (rp g) t m", g=N_GROUPS, t=PACK),
        )

        load_labels(6)
        for rp in range(R_PASSES):
            round_a(1, rp)
        for rp in range(R_PASSES):
            quantise_a(1, rp)
        load_labels(7)

        for rp in range(R_PASSES):
            for t in range(PACK):
                cols = slice(t * P, (t + 1) * P)
                logits = psum.tile([P, S], F32, name="bank")
                for kp in range(K_PASSES):
                    nc.tensor.matmul_mx(
                        logits[:],
                        lhsT=a_codes[kp, rp][:, cols].bitcast(FP8X4),
                        lhsT_scale=a_planes[kp, rp][:, cols],
                        rhs=v_codes[kp][:].bitcast(FP8X4),
                        rhs_scale=v_planes[QUAD_ROWS * (1 + kp) : P, :],
                        start=(kp == 0),
                        stop=(kp == K_PASSES - 1),
                    )
                for cols in HALVES if (rp, t) == (LAST, 0) else WHOLE:
                    name = "prob%d%d" % (rp, t) if cols.start == 0 else "prob_rest"
                    part = keep.tile([P, cols.stop - cols.start], F32, name=name, align_bytes=64)
                    nc.scalar.activation(part[:], logits[:, cols], ACT.Sigmoid, bias=bias[:, t, rp : rp + 1])
                    prob[rp, t, cols.start] = part

        d_round = {LAST: keep.tile([P, S, PACK], BF16, name="d_round%d" % LAST, align_bytes=64)}
        d_pairs = [keep.tile([P, 2, S, 2], BF16, name="d_pairs%d" % rp, align_bytes=64) for rp in range(LAST)]
        y_banks = [psum.tile([P, S], F32, name="bank") for bank_no in range(N_GROUPS * PACK)]

        def weave(rp):
            d_round[rp] = keep.tile([P, S, PACK], BF16, name="d_round%d" % rp, align_bytes=64)
            nc.scalar.copy(
                d_round[rp][:].rearrange("p j t -> p (j t)").bitcast(U32).rearrange("p (j u) -> p j u", u=2),
                d_pairs[rp][:].rearrange("p u j e -> p (u j e)").bitcast(U32).rearrange("p (u j) -> p j u", u=2),
            )

        second = {}

        def row_gradient(rp, t):
            scale = minus_weight[:, t, rp : rp + 1]
            miss = ring.tile([P, S], F32, name="miss", bufs=MISS_BUFS)
            pieces = LAST_PIECES[t] if rp == LAST else WHOLE
            if (rp, t + 1) in loads[1 : 2 * PAIRS : 2]:
                second[rp, t + 1] = ring.tile([P, S], F32, name="second")
                nc.vector.tensor_copy(second[rp, t + 1][:], label_rows[rp, t][:, T:].indirect(offsets[:]))
            if (rp, t) in second:
                nc.vector.tensor_tensor(miss[:], second[rp, t][:], prob[rp, t, 0][:], ALU.subtract)
            for cols in pieces if (rp, t) in label_rows else ():
                picked = label_rows[rp, t][:].indirect(offsets[:, cols.start // 16 : cols.stop // 16])
                part = prob[rp, t, cols.start][:] if (rp, t) == (LAST, 0) else prob[rp, t, 0][:, cols]
                nc.vector.tensor_tensor(miss[:, cols], picked, part, ALU.subtract)
            for cols in pieces:
                place = d_round[rp][:, cols, t] if rp == LAST else d_pairs[rp][:, t // 2, cols, t % 2]
                nc.scalar.activation(place, miss[:, cols], ACT.Copy, scale=scale)

        d_codes, d_plane, late_raw = {}, {}, {}
        wb_plane = {rp: wb_planes[:, rp, :] for rp in range(LAST)}

        def load_last_words():
            late_raw[LAST] = keep.tile([P, 2 * N], U8, name="late_raw", tag="prob11", align_bytes=64)
            nc.sync.dma_start(late_raw[LAST][:].bitcast(I32), wb_words[LAST].bitcast(I32))
            last_plane = keep.tile([P, N], U8, name="last_plane", tag="prob13", align_bytes=64)
            for quad in range(QUADS):
                nc.sync.dma_start(
                    last_plane[32 * quad : 32 * quad + QUAD_ROWS, :].bitcast(I32),
                    wb_planes[32 * quad + QUAD_ROWS : 32 * (quad + 1) : PARK_STEP, 0, :].bitcast(I32),
                )
            wb_plane[LAST] = last_plane[:]

        def quantise_d(rp, span, after):
            codes = keep.tile([P, span.stop - span.start], U32, name="d_codes", tag="prob%d%d" % after, align_bytes=64)
            for q in range(span.start // P, span.stop // P):
                d_codes[rp, q] = (codes, span.start)
            if span.start == 0:
                d_plane[rp] = keep.tile([P, S], U8, name="d_plane%d" % rp, align_bytes=64)
            for piece, cols in enumerate(QUARTERS if rp == LAST else (span,)):
                if rp == LAST and piece % 2 == 0:
                    deal_words(LAST, late_raw[LAST][:], piece, 2, "last_codes%d" % piece)
                nc.vector.quantize_mx(
                    codes[:, cols.start - span.start : cols.stop - span.start].bitcast(FP8X4),
                    d_plane[rp][:, cols],
                    d_round[rp][:, cols, :].rearrange("p j t -> p (j t)"),
                )
            if rp == LAST:
                deal_words(LAST, late_raw[LAST][:], PACK, PACK, "d_round%d" % LAST)

        def back_project(rp, span):
            first = rp == 0

            def one_pass(out, rows_no, cols, start, stop):
                codes, begin = d_codes[rp, cols.start // P]
                nc.tensor.matmul_mx(
                    out,
                    lhsT=wb_codes[rp, rows_no].bitcast(FP4X4),
                    lhsT_scale=wb_plane[rp][:, P * rows_no : P * (rows_no + 1)],
                    rhs=codes[:, cols.start - begin : cols.stop - begin].bitcast(FP8X4),
                    rhs_scale=d_plane[rp][:, cols],
                    start=start,
                    stop=stop,
                )

            for half in range(2):
                for pair in range(2):
                    for q in range(2):
                        for row in range(2 if span.start <= QUARTERS[2 * half + q].start < span.stop else 0):
                            place = row * HALF + q * P
                            one_pass(
                                y_banks[2 * half + pair][:, place : place + P],
                                2 * pair + row,
                                QUARTERS[2 * half + q],
                                first and q == 0 and row == 0,
                                rp == LAST and q == 1 and row == 1,
                            )
            for bank_no in range(PACK, PSUM_BANKS):
                for cols in {S: WHOLE, 3 * P: (HALVES[0], QUARTERS[2]), P: QUARTERS[3:]}[span.stop - span.start]:
                    one_pass(y_banks[bank_no][:, cols], bank_no, cols, first, rp == LAST)

        closing = {(1, 2): (0, WHOLE[0]), (LAST, 1): (1, slice(0, 3 * P)), (LAST, 2): (1, QUARTERS[3]), (LAST, 3): (LAST, WHOLE[0])}
        for step, (rp, t) in enumerate(loads):
            row_gradient(rp, t)
            for later in {0: (8,), 1: (9,), 2: (10,), 4: (11,)}.get(step, ()):
                load_labels(later)
            if (rp, t) == (1, 3):
                load_last_words()
            if rp < LAST and t == PACK - 1:
                weave(rp)
            if (rp, t) in closing:
                quantise_d(*closing[rp, t], (rp, t))
                back_project(*closing[rp, t])

        y_planes = keep.tile([P, N_GROUPS, S], U8, name="y_planes", align_bytes=64)
        y, y_round, y_early = [], [], []

        def empty_banks(g):
            y.append(keep.tile([P, PACK, S], F32, name="y", tag="wide%d" % g, align_bytes=64))
            rows = out_0[g * PASS : (g + 1) * PASS, :].rearrange("(p t) j -> p t j", t=PACK)
            for t in range(PACK):
                bank = y_banks[g * PACK + t]
                if g == 0 and t % 2 == 0:
                    cols = HALVES[t // 2]
                    for row in range(2):
                        nc.scalar.copy(y[g][:, row, cols], bank[:, HALVES[row]])
                        nc.sync.dma_start(rows[:, row, cols], y[g][:, row, cols])
                elif g == 0:
                    nc.vector.tensor_copy(y[g][:, 2:, HALVES[t // 2]], bank[:].rearrange("p (row j) -> p row j", row=2))
                elif t < 2:
                    nc.vector.tensor_copy(y[g][:, t, :], bank[:])
                else:
                    nc.scalar.copy(y[g][:, t, :], bank[:])
                if (g, t) == (0, 3):
                    nc.sync.dma_start(rows[:, t - 1 : t + 1, :], y[g][:, t - 1 : t + 1, :])
                if (g, t) == (1, 3):
                    nc.sync.dma_start(rows, y[g][:])

        def round_y(g):
            y_round.append(ring.tile([P, S, PACK], BF16, name="y_round", tag="round", bufs=ROUND_BUFS, align_bytes=64))
            split = S if g == 0 else VECTOR_ROUNDS
            first = HALF if g == 0 else 0
            if g == 0:
                y_early.append(keep.tile([P, HALF, PACK], BF16, name="y_early", tag="prob11", align_bytes=64))
                columns = y[g][:, :, :HALF].rearrange("p t j -> p j t")
                nc.gpsimd.tensor_scalar(y_early[0][:], columns, 1.0, 0.0, ALU.mult, ALU.add)
            nc.vector.tensor_copy(
                y_round[g][:, first:split, :].rearrange("p (run near) t -> p run t near", near=NEAR),
                y[g][:, :, first:split].rearrange("p t (run near) -> p run t near", near=NEAR),
            )
            for cols in () if g == 0 else QUARTERS[VECTOR_ROUNDS // P :]:
                nc.scalar.copy(
                    y_round[g][:, cols, :].rearrange("p (run near) t -> p run t near", near=NEAR),
                    y[g][:, :, cols].rearrange("p t (run near) -> p run t near", near=NEAR),
                )

        def quantise_y(g):
            y_codes = keep.tile([P, S], U32, name="y_codes%d" % g, align_bytes=64)
            words = out_1[g].rearrange("p j t -> p (j t)").bitcast(I32)
            for cols in HALVES if g == 0 else (HALVES[0],) + QUARTERS[2:]:
                rounded = y_early[0][:] if (g, cols.start) == (0, 0) else y_round[g][:, cols, :]
                nc.vector.quantize_mx(
                    y_codes[:, cols].bitcast(FP8X4),
                    y_planes[:, g, cols],
                    rounded.rearrange("p j t -> p (j t)"),
                )
            nc.sync.dma_start(words, y_codes[:].bitcast(I32))

        for stage in (empty_banks, round_y, quantise_y):
            for g in range(N_GROUPS):
                stage(g)
        for quad in range(QUADS):
            nc.scalar.dma_start(
                out_2[:, QUAD_ROWS * quad : QUAD_ROWS * (quad + 1), :].rearrange("g row j -> row g j").bitcast(I32),
                y_planes[32 * quad : 32 * quad + QUAD_ROWS, :, :].bitcast(I32),
            )
